import numpy as np, ml_dtypes
CORES = [48,51,52,55]
N = 4
import mx_ref
BF = ml_dtypes.bfloat16
def entries(a):
    return np.ascontiguousarray(a.T).reshape(-1)
def table(e):
    return np.ascontiguousarray(np.reshape(e, (-1, 16)).T).astype(np.int32)
def gcols(t, e):
    v = np.concatenate([t.reshape(8, 16, -1, 4), np.zeros((8, 16, 1, 4), BF)], axis=2)
    return np.ascontiguousarray(np.stack([v[g][:, e[g]] for g in range(8)])).reshape(128, -1)
def gpick(z, e):
    return np.concatenate([z[16 * g:16 * g + 16][:, e[g]] for g in range(8)])
def tile(rs):
    return np.stack(rs, axis=2).reshape(128, -1).astype(BF)
def pick(q, e):
    c = np.concatenate([q[0].reshape(128, -1, 4), np.zeros((128, 1, 4), np.uint8)], axis=1); s = np.concatenate([q[1], np.ones((16, 1), np.uint8)], axis=1)
    return (np.ascontiguousarray(c[:, e].reshape(128, -1)), np.ascontiguousarray(s[:, e]))
def join(*qs):
    return (np.concatenate([q[0] for q in qs], axis=1), np.concatenate([q[1] for q in qs], axis=1))
def put(q, e, v):
    c, s = q[0].reshape(128, -1, 4).copy(), q[1].copy(); c[:, e] = v[0].reshape(128, -1, 4); s[:, e] = v[1]
    return (c.reshape(128, -1), s)
def pk(c, s):
    return (np.ascontiguousarray(c), mx_ref.live(s))
def emit(q):
    return q[0], q[1]
def packed(v, rng):
    q = [mx_ref.quantize(np.ascontiguousarray(v[r])) for r in range(N)]
    return np.stack([a for a, b in q]), np.stack([mx_ref.plane(b, rng) for a, b in q])
def values_of_codes():
    e, c = np.zeros((128, 128, 4), np.float32), np.zeros((128, 2, 4), np.uint8)
    e[np.arange(128), np.arange(128), 0] = 1
    c[:127, :, 0] = np.arange(256).reshape(2, 128).T[:127]
    return mx_ref.matmul(mx_ref.quantize(e.reshape(128, 512).astype(BF)), (c.reshape(128, 8), np.full((16, 2), 127, np.uint8))).T.reshape(-1).astype(np.float64)
CODE_VALUE, SCALE_VALUE = values_of_codes(), 2.0 ** (np.arange(256) - 127.0)
def decode(q):
    return (CODE_VALUE[q[0]].reshape(16, 8, -1, 4) * SCALE_VALUE[q[1]][:, None, :, None] + 0.0).reshape(128, -1).astype(np.float32)
def f(rng, *shape):
    return mx_ref.flush((rng.standard_normal(shape, dtype=np.float32) * np.exp2(rng.integers(-2, 3, shape[:-1] + (1,)))).astype(BF))
def wide(rng, *shape, cols=0):
    v = rng.standard_normal(shape, dtype=np.float32) * np.exp2(rng.integers(-12, 13, shape)).astype(np.float32)
    if cols: v *= np.repeat(np.exp2(rng.integers(-cols, cols + 1, shape[:-2] + (1, shape[-1] // 4))) * (rng.random(shape[:-2] + (1, shape[-1] // 4)) > 0.0625), 4, axis=-1).astype(np.float32)
    return mx_ref.flush(v.astype(BF))
C, H, R = 512, 256, 3
WIDTH = [2, 4, 8, 16, 32, 64, 128, 256]
def big(v):
    v = v.astype(np.float32)
    v[np.abs(v) < np.float32(2.0 ** -16)] = 0
    return v.astype(BF)
def numbers_of(rng):
    return {"x": big(f(rng, N, 128, 4 * C)), "u": np.array(f(rng, N, 128, 512)), "v": np.array(f(rng, N, 128, 512))}
def bases(rng):
    return np.stack([table(rng.permutation(C)) for r in range(N)])
def layers(rng):
    return big(f(rng, N, 128, 2048)).reshape(N, 8, 16, 4, 8, 16, 4)
def weights(rng, w):
    c, s = packed(np.ascontiguousarray(w).reshape(N, 128, 2048), rng)
    return {"wc": c, "ws": s}
def setup_inputs(rng):
    return {**numbers_of(rng), "p": bases(rng), **weights(rng, layers(rng))}
def setup_inputs_ties(rng):
    d = numbers_of(rng)
    p = bases(rng)
    o = rng.permutation(N)
    x = d["x"].astype(np.float32).reshape(N, 8, 16, C, 4)
    n = (N, 8, 8, C, 4)
    x[:, :, 8:] = (1.125 + 0.25 * rng.integers(0, 4, n)) * np.exp2(-1.0 * rng.integers(8, 15, n)) * rng.choice([-1.0, 1.0], n)
    x[:, :, 8, :, 0] = 1.96875
    x[:, :, :8] = 0
    u = d["u"].reshape(N, 128, 128, 4)
    u[:, :, ::16] = 0
    for r in range(N):
        if o[r] % 2 == 1: x[r, :, 0, :, 0] = rng.integers(0, 4, (8, C))
        else: x[r, :, 0, :, 0] = rng.integers(0, 7, (1, C)) + rng.integers(0, 2, (8, C))
        for h in range(0, 128, 16): u[r, h, h, 0] = 0.0 if o[r] == 0 else -1.0 if o[r] == 1 else 1.0
        if o[r] == 0:
            x[r, 7, 0, :, 0] = 0
            x[r, 7, 0, p[r, 0, 0], 0] = 1
            u[r, 112, 112, 0] = 1.0
    w = layers(rng)
    w[:, :, :, :, :, :8] = 0
    return {"x": x.reshape(N, 128, 4 * C).astype(BF), "u": u.reshape(N, 128, 512), "v": d["v"], "p": p, **weights(rng, w)}
def setup_inputs_near(rng):
    d = numbers_of(rng)
    x = d["x"].astype(np.float32).reshape(N, 8, 16, C, 4)
    u = d["u"].reshape(N, 128, 128, 4)
    o = rng.permutation(N) % 4
    x[:, :, 0] = 0
    x[:, :, 8:] = 0
    u[:, :, ::16] = 0
    for r in range(N):
        k = 1.0 if o[r] == 0 else 2.0 ** -30
        if o[r] < 3:
            s = rng.integers(0, 252, (1, C)) + rng.integers(0, 4, (8, C))
            for i in range(2): x[r, :, 8 + i] = ((s[:, :, None] >> (4 * i + np.arange(4))) & 1) * np.exp2(4 * i + np.arange(4) - 23.0)
            if o[r] < 2:
                x[r, :, 0, :, 0] = rng.choice([-1.0, 1.0], C)
                x[r, :, 11, :, 0] = 2.0 ** -10
            for g in rng.permutation(8)[:4]: x[r, g, 0, rng.integers(C), 0] = 2.0 ** 29 * rng.choice([-1.0, 1.0])
        else:
            for i in (10, 12): x[r, :, i, :, 0] = (1.0 + 0.125 * rng.integers(0, 2, (8, C))) * 2.0 ** -30
        for h in range(0, 128, 16):
            if o[r] < 3:
                u[r, h, h, 0] = k
                u[r, h + 8:h + 10, h] = k
                u[r, h + 11, h, 0] = k
            else:
                a = rng.choice([-1.0, 1.0])
                u[r, h + 10, h, 0] = 1.125 * k * a
                u[r, h + 12, h, 0] = -k * a
    w = layers(rng)
    for i in (0, 8, 9, 10, 11, 12, 13, 14, 15):
        w[:, :, i] = 0
        w[:, :, :, :, :, i] = 0
    return {"x": x.reshape(N, 128, 4 * C).astype(BF), "u": u.reshape(N, 128, 512), "v": d["v"], "p": bases(rng), **weights(rng, w)}
def setup_inputs_huge(rng):
    d = numbers_of(rng)
    o = rng.permutation(N)
    x = 0.6 + 0.06 * rng.random((N, 8, 16, C, 4)) + 0.03 * rng.random((N, 1, 1, C, 1))
    a = 1.0 - 0.1 * rng.random((N, 128, 8, 4))
    for r in range(N):
        if o[r] < N // 2: a[r] *= -1.0
        else:
            x[r] *= rng.choice([-1.0, 1.0], (1, 1, C, 1))
            a[r] *= rng.choice([-1.0, 1.0], (1, 8, 1))
    u = d["u"].reshape(N, 128, 128, 4)
    u[:, :, ::16] = (2.0 ** 30 * a).astype(np.float32).astype(BF)
    w = np.zeros((N, 128, 4, 128, 4), np.float32)
    i = np.arange(128)
    for b in range(4): w[:, i, b, i, b] = -4
    return {"x": (2.0 ** 30 * x).astype(np.float32).reshape(N, 128, 4 * C).astype(BF), "u": u.reshape(N, 128, 512), "v": d["v"], "p": bases(rng), **weights(rng, w.astype(BF))}
def setup_inputs_ends(rng):
    v = np.array(f(rng, N, 128, 512))
    o = rng.permutation(N) % 4
    x, u = np.zeros((N, 128, C, 4), np.float32), np.zeros((N, 128, 128, 4), np.float32)
    w, e = np.zeros((N, 128, 4, 128, 4), np.float32), []
    i = np.arange(128)
    for r in range(N):
        c = rng.choice([-1.0, 1.0], (1, C, 1))
        a = rng.choice([-1.0, 1.0], (1, 128, 1))
        if o[r] == 0:
            x[r] = 2.0 ** 30
            x[r, 64:] *= rng.choice([0.5, 1.0], (64, C, 4))
            x[r, 64:, ::4] = 2.0 ** 30
            u[r] = -2.0 ** 30
            u[r, 64:, :64] = 0
        elif o[r] == 1:
            x[r] = 2.0 ** 30 * c
            u[r] = 2.0 ** 30 * a
        elif o[r] == 2:
            x[r] = 2.0 ** -29 * rng.choice([-1.0, 1.0], (128, C, 4))
            u[r] = 2.0 ** -30 * rng.choice([-1.0, 1.0], (128, 128, 4))
        else:
            x[r] = 2.0 ** -29 * c
            u[r] = 2.0 ** -30 * a
        if o[r] > 1:
            for b in range(4): w[r, i, b, i, b] = 2.0 ** -20
        e.append(table(np.arange(C) if o[r] % 2 == 0 else C - 1 - np.arange(C)))
    v = (np.where(v < 0, -1.0, 1.0) * np.where(rng.permutation(N) % 2, 2.0 ** -30, 2.0 ** 30)[:, None, None]).astype(np.float32).astype(BF)
    return {"x": x.reshape(N, 128, 4 * C).astype(BF), "u": u.reshape(N, 128, 512).astype(BF), "v": v, "p": np.stack(e), **weights(rng, w.astype(BF))}
def setup_inputs_spread(rng):
    d = setup_inputs(rng)
    d["x"] = big(wide(rng, N, 128, 4 * C, cols=6))
    return d
def check_inputs(d):
    bad = []
    for k in ("x", "u", "v"):
        a = np.abs(d[k].astype(np.float32))
        if not (np.isfinite(a).all() and ((a == 0) | (a >= 2.0 ** -30) & (a <= 2.0 ** 30)).all()): bad.append("a value of " + k)
    none, least, most = [emit(mx_ref.quantize(np.full((128, 16), k, np.float32).astype(BF)))[1][0, 0] for k in (0.0, 2.0 ** -30, 2.0 ** 30)]
    for r in range(N):
        if not np.array_equal(np.sort(d["p"][r].reshape(-1)), np.arange(C)): bad.append("p: not every column once")
        if ((d["wc"][r] == 0x7F) | (d["wc"][r] == 0xFF)).any(): bad.append("wc: a code that is no number")
        s = mx_ref.live(d["ws"][r])
        if ((s != none) & ((s < least) | (s > most))).any(): bad.append("ws: a scale out of range")
    return bad
def reference(x, u, v, p, wc, ws):
    qu = [mx_ref.quantize(u[r]) for r in range(N)]
    lay = [pk(wc[r], ws[r]) for r in range(N)]
    now = [x[r] for r in range(N)]
    base = [entries(p[r]) for r in range(N)]
    order = np.zeros((N, 8, C), np.int64)
    for t in range(R):
        own, sent = [], []
        for r in range(N):
            q = mx_ref.quantize(now[r])
            own.append(decode(q))
            s = mx_ref.matmul(qu[r], q)[::16] + np.float32(0.0)
            o = base[r]
            for g in range(8):
                key = np.maximum.accumulate(s[g][o].reshape(-1, WIDTH[g]), axis=1).reshape(-1, 2 * WIDTH[g])
                o = np.take_along_axis(o.reshape(-1, 2 * WIDTH[g]), np.argsort(key, axis=1, kind="stable"), axis=1).reshape(-1)
                order[r, g] = o
            base[r] = o
            a = own[r].astype(BF)
            z = (gcols(a, order[r, :, :H]).astype(np.float32) + gcols(a, order[r, :, H:]).astype(np.float32)) * np.float32(0.5)
            sent.append(mx_ref.quantize(z.astype(BF)))
        for r in range(N):
            q = sent[(r - 1) % N]
            place = np.argsort(order[r], axis=1) % H
            now[r] = tile([gpick(mx_ref.matmul(pick(lay[r], np.arange(128 * b, 128 * b + 128)), q), place) * np.float32(0.03125) + own[r][:, b::4] for b in range(4)])
    y, od = np.zeros((N, 128, C), np.float32), np.zeros((N, 8, C), np.float32)
    oc, osc = np.zeros((N, 128, 4 * C), np.uint8), np.zeros((N, 16, C), np.uint8)
    for r in range(N):
        q = mx_ref.quantize(now[r])
        y[r] = mx_ref.matmul(mx_ref.quantize(v[r]), q)
        od[r] = order[r]
        oc[r], osc[r] = emit(q)
    return {"y": y, "od": od, "oc": oc, "osc": osc}

@@ -1,0 +1,559 @@
+from concourse.mybir import dt, AluOpType as OP, ActivationFunctionType as AF
+
+BIG = 2.0 ** 75
+SEP = 64.0
+DIG = 2.0 ** 14
+R = 3
+
+SCRATCH = {}
+PLACE = {}
+_used = {"ar": 0, "ar16": 0}
+SEMAPHORES = ["sv", "ss", "sp", "sg", "dx0", "dx1", "du", "dv", "dp", "dw", "doc", "dos", "dod", "dy"]
+
+
+def _buf(name, cols, dtype="float32", where="sbuf"):
+    SCRATCH[name] = (where, [128, cols], dtype)
+    PLACE[name] = (name, 0, cols)
+
+
+def _part(name, cols, arena="ar"):
+    PLACE[name] = (arena, _used[arena], cols)
+    _used[arena] += -(-cols // 16) * 16
+
+
+for _n, _c in (("n16", 512), ("i17", 68), ("iot", 512), ("iotm", 512), ("io4", 4), ("bff", 16), ("sg", 6), ("sgk", 24), ("rtab", 4),
+               ("mh", 64), ("md", 512), ("mda", 512), ("t1", 64), ("t2", 64), ("t3", 68), ("msk3", 68), ("msk4", 132),
+               ("c0", 68), ("c1", 68), ("c2", 68), ("c3", 68), ("c4", 132), ("c5", 260), ("c6", 516), ("c7", 1028),
+               ("kk", 64), ("gm", 64), ("kd", 64), ("kds", 4), ("sm", 132), ("ko", 256), ("kp", 256), ("gg", 512), ("hh", 64),
+               ("jk", 260), ("sum4", 4), ("sh", 32), ("aa", 32), ("a5", 8), ("ap6", 32), ("tr", 32), ("sw", 32), ("tr2", 32), ("tr7", 32), ("x7", 32), ("l7", 32),
+               ("id6", 64), ("id7", 64), ("posw", 512), ("pds", 512), ("lr", 20), ("tbf", 4), ("idw", 64), ("ds", 512)):
+    _part(_n, _c)
+for _g in range(5):
+    for _s in ("g%d", "o%d", "id%dr", "rst%d"):
+        _part(_s % _g, 64)
+for _g in range(3):
+    _part("mq%d" % _g, 64)
+    _part("ms%d" % _g, 68)
+for _r in range(R):
+    _part("list%d" % _r, 32)
+    for _g, _c in ((5, 128), (6, 256), (7, 512)):
+        _part("w%d%d" % (_g, _r), _c)
+    SCRATCH["dg%d" % _r] = ("dram", [5, 128, 4], "float32")
+for _n, _c in (("uo", 64), ("rk", 4), ("tb", 4), ("tab5", 8), ("tab6", 16), ("tab7", 32), ("own6", 4), ("own7", 4), ("off", 32), ("pos", 32),
+               ("tbl0", 4), ("tbl1", 4), ("tbl2", 4), ("tbl3", 4)):
+    _part(_n, _c, "ar16")
+_buf("ar", _used["ar"])
+_buf("ar16", _used["ar16"], "uint16")
+_buf("row", 512)
+_buf("yy", 512)
+for _g in range(8):
+    _buf("sw%d" % _g, 512)
+for _b in range(4):
+    _buf("fh%d" % _b, 512)
+    _buf("pa%d" % _b, 256)
+    _buf("pp%d" % _b, 256)
+for _b in range(2):
+    _buf("f%d" % _b, 512)
+    _buf("gp%d" % (_b + 2), 512)
+for _n, _c in (("pi", 1), ("bi", 16), ("uoi", 64), ("tbi", 4)):
+    _buf(_n, _c, "int32")
+for _n, _c in (("xt", 2048), ("ut", 512), ("vt", 512), ("zt", 1024), ("ee", 2048), ("ones", 512)):
+    _buf(_n, _c, "bfloat16")
+for _n, _c in (("xq", 512), ("uq", 128), ("uc", 1024), ("vq", 128), ("wq", 512), ("zq", 256), ("eq", 512)) + tuple(("zl%d" % r, 256) for r in range(R)):
+    _buf(_n, _c, "float8_e4m3fn_x4")
+    _buf(_n + "s", _c, "uint8")
+for _b in range(8):
+    _buf("b%d" % _b, 512, "float32", "psum")
+for _r in range(R):
+    SEMAPHORES += [s % _r for s in ("ac%d", "as%d", "lc%d", "ls%d", "dl%d", "dm%d", "dn%d", "db%d")]
+    SEMAPHORES += ["dga%d%d" % (_r, g) for g in range(5)]
+
+
+def rank_program(g, core, T, topo):
+    rank = T.rank_of(core)
+    if rank is None:
+        return
+    nxt = T.cores[(rank + 1) % len(T.cores)]
+    queues = {"v": g.vector, "s": g.scalar, "t": g.tensor, "g": g, "y": g.sync}
+    semof = {"v": "sv", "s": "ss", "t": "sp", "g": "sg"}
+    count = {k: 0 for k in semof}
+    known = {k: {} for k in queues}
+    hist = {}
+    total = {}
+
+    def need(q, tok):
+        sem, val = tok
+        if known[q].get(sem, 0) < val:
+            queues[q].wait_ge(T.sem[sem], val)
+            known[q][sem] = val
+
+    def v(name, c0=0, c1=None, st=1, p0=0, p1=128):
+        name, at, cols = PLACE[name]
+        c0, c1 = c0 + at, (cols if c1 is None else c1) + at
+        ap = T[name][p0:p1, c0:c1] if st == 1 else T[name][p0:p1, c0:c1:st]
+        return (name, p0, p1, c0, c1, ap)
+
+    def deps(q, ins, outs):
+        toks = {}
+        for w, views in ((0, ins), (1, outs)):
+            for n, p0, p1, c0, c1, ap in views:
+                ps = n in SCRATCH and SCRATCH[n][0] == "psum"
+                for (tok, eng, hw, a, b, c, d) in hist.get(n, []):
+                    if ps and eng != q or (w or hw) and a < p1 and p0 < b and c < c1 and c0 < d:
+                        toks[tok[0]] = max(toks.get(tok[0], 0), tok[1])
+        for s in sorted(toks):
+            need(q, (s, toks[s]))
+
+    def note(q, tok, ins, outs):
+        for w, views in ((0, ins), (1, outs)):
+            for n, p0, p1, c0, c1, ap in views:
+                h = hist.setdefault(n, [])
+                if w:
+                    h[:] = [e for e in h if not (p0 <= e[3] and e[4] <= p1 and c0 <= e[5] and e[6] <= c1)]
+                else:
+                    h[:] = [e for e in h if not (e[1] == q and not e[2] and e[0][0] == tok[0] and e[3:] == (p0, p1, c0, c1))]
+                h.append((tok, q, w, p0, p1, c0, c1))
+
+    def op(q, fn, outs, ins):
+        deps(q, ins, outs)
+        i = fn(queues[q])
+        count[q] += 1
+        i.then_inc(T.sem[semof[q]], 1)
+        note(q, (semof[q], count[q]), ins, outs)
+
+    def dma(q, sem, group, out, in_):
+        deps(q, [in_], [out])
+        queues[q].dma_start(out[5], in_[5]).then_inc(T.sem[sem], 16)
+        total[sem] = 16 * group
+        note(q, (sem, 16 * group), [in_], [out])
+
+    def cd(name):
+        n, p0, p1, a, b, ap = v(name)
+        return (n, p0, p1, a, b, ap.bitcast(dt.uint8))
+
+    def ts(out, in0, s1, op0, s2=None, op1=None):
+        ins = [in0] + [s for s in (s1, s2) if isinstance(s, tuple)]
+        a, b = [s[5] if isinstance(s, tuple) else s for s in (s1, s2)]
+        if op1 is None:
+            op("v", lambda e: e.tensor_scalar(out[5], in0[5], a, None, op0), [out], ins)
+        else:
+            op("v", lambda e: e.tensor_scalar(out[5], in0[5], a, b, op0, op1), [out], ins)
+
+    def tt(out, a, b, o):
+        op("v", lambda e: e.tensor_tensor(out[5], a[5], b[5], o), [out], [a, b])
+
+    def ttg(out, win, off, b):
+        op("v", lambda e: e.tensor_tensor(out[5], win[5].indirect(off[5]), b[5], OP.add), [out], [win, off, b])
+
+    def scan(out, d0, d1, init, o0, o1):
+        op("v", lambda e: e.tensor_tensor_scan(out[5], d0[5], d1[5], init, o0, o1), [out], [d0, d1])
+
+    def copy(out, in_):
+        op("v", lambda e: e.tensor_copy(out[5], in_[5]), [out], [in_])
+
+    def trans(out, in_):
+        op("v", lambda e: e.transpose(out[5], in_[5]), [out], [in_])
+
+    def fill(out, c):
+        op("v", lambda e: e.memset(out[5], c), [out], [])
+
+    def vgather(out, win, off):
+        op("v", lambda e: e.tensor_copy(out[5], win[5].indirect(off[5])), [out], [win, off])
+
+    def scatter(win, off, in_):
+        op("v", lambda e: e.tensor_copy(win[5].indirect(off[5]), in_[5]), [win], [off, in_])
+
+    def act(out, in_, scale=1.0):
+        op("s", lambda e: e.activation(out[5], in_[5], AF.Copy, scale=scale), [out], [in_])
+
+    def sgather(out, win, off):
+        op("s", lambda e: e.activation(out[5], win[5].indirect(off[5]), AF.Copy), [out], [win, off])
+
+    def accum(out, in_, acc):
+        op("s", lambda e: e.activation(out[5], in_[5], AF.Copy, accum_out=acc[5]), [out, acc], [in_])
+
+    def quant(c, s, t):
+        op("v", lambda e: e.quantize_mx(c[5], s[5], t[5]), [c, s], [t])
+
+    def mm(out, l, ls, r_, rs):
+        op("t", lambda e: e.matmul_mx(out[5], l[5], ls[5], r_[5], rs[5], True, True), [out], [l, ls, r_, rs])
+
+    def iota(out, pat, base=0, cm=0):
+        if out[0] in ("pi", "uoi"):
+            op("g", lambda e: e.iota(out[5], pat, base, cm), [out], [])
+        else:
+            op("g", lambda e: e.iota(out[5], pat, base, cm, allow_small_or_imprecise_dtypes=True), [out], [])
+
+    def group_of(B):
+        return 2 * (B % 4) + B // 4
+
+    dma("y", "du", 1, v("ut"), ("u", 0, 128, 0, 512, T.u[:, :]))
+    dma("s", "dx0", 1, v("xt", 0, 1024), ("x", 0, 128, 0, 1024, T.x[:, 0:1024]))
+    dma("y", "dx1", 1, v("xt", 1024, 2048), ("x", 0, 128, 1024, 2048, T.x[:, 1024:2048]))
+    for B in range(8):
+        h = 16 * group_of(B)
+        dma("y", "dp", 8, v("tbi", 0, 4, 1, h, h + 16), ("p", 0, 16, 4 * B, 4 * B + 4, T.p[:, 4 * B:4 * B + 4]))
+    dma("y", "dv", 1, v("vt"), ("v", 0, 128, 0, 512, T.v[:, :]))
+    dma("y", "dw", 2, cd("wq"), ("wc", 0, 128, 0, 2048, T.wc[:, :]))
+    dma("y", "dw", 2, v("wqs"), ("ws", 0, 128, 0, 512, T.ws[:, :]))
+
+    iota(v("uoi"), [[16, 8], [0, 8]])
+    iota(v("pi"), [[0, 1]], 0, 1)
+    iota(v("n16", 0, 64), [[0, 4], [1, 16]])
+    iota(v("io4"), [[16, 4]])
+    iota(v("i17"), [[0, 4], [1, 17]])
+    iota(v("iot"), [[1, 512]])
+    fill(v("ones"), 1.0)
+    for b in range(4):
+        o, i = v("ee", 512 * b, 512 * b + 512), v("ones")
+        op("g", lambda e: e.affine_select(o[5], i[5], [[-1, 512]], OP.is_equal, 0.0, b, 4), [o], [i])
+    iota(v("n16", 64, 512), [[0, 28], [1, 16]])
+    for r in range(R):
+        for k, c in ((5, 128), (6, 256), (7, 512)):
+            iota(v("w%d%d" % (k, r)), [[0, c]])
+    iota(v("iotm"), [[0, 2], [1, 256]])
+
+    copy(v("uo"), v("uoi"))
+    for j, m in enumerate((15, 2, 4, 8, 32, 64, 16, 14, 12)):
+        ts(v("bi", j, j + 1), v("pi"), m, OP.bitwise_and)
+    ts(v("bi", 9, 10), v("pi"), 4, OP.arith_shift_right)
+    copy(v("bff", 0, 10), v("bi", 0, 10))
+    q = v("bff", 0, 1)
+    quant(v("uq"), v("uqs"), v("ut"))
+
+    def upick(a, b):
+        o, w, f = v("uc", 128 * a, 128 * b), v("uq"), v("uo", 8 * a, 8 * b)
+        op("v", lambda e: e.tensor_copy(o[5].bitcast(dt.uint32), w[5].bitcast(dt.uint32).indirect(f[5])), [o], [w, f])
+        sgather(v("ucs", 128 * a, 128 * b), v("uqs"), f)
+
+    upick(0, 1)
+    sgn = {}
+    for i, (k, c, m) in enumerate(((0, 1, 2), (1, 2, 4), (2, 3, 8), (5, 4, 32), (6, 5, 64), (7, 6, 16))):
+        sgn[k] = v("sg", i, i + 1)
+        ts(sgn[k], v("bff", c, c + 1), -2.0 / m, OP.mult, 1.0, OP.add)
+    col = [0]
+
+    def newcol():
+        col[0] += 1
+        return v("sgk", col[0] - 1, col[0])
+
+    dsc, m7, q1 = newcol(), newcol(), newcol()
+
+    def dscp(a, b):
+        return v("sgk", 0, 1, 1, a, b)
+
+    ts(dsc, q, 15.0, OP.is_equal, 1.0 - 1.0 / DIG, OP.mult)
+    ts(q1, q, 1.0, OP.add)
+    ts(v("rtab"), v("io4"), q, OP.add)
+    ts(dsc, dsc, 1.0 / DIG, OP.add)
+    sgb = {}
+
+    def small(k):
+        w = 2 << k
+        fill(v("rst%d" % k), BIG)
+        lo = v("bff", (7, 8, 3)[k], (7, 8, 3)[k] + 1)
+        rs, rw, bs, b8 = newcol(), newcol(), newcol(), newcol()
+        sgb[k] = newcol()
+        ts(sgb[k], sgn[k], 1.0 / SEP, OP.mult)
+        ts(rs, sgn[k], float(w), OP.mult, lo, OP.add)
+        ts(bs, sgn[k], SEP, OP.mult)
+        ts(b8, sgn[k], 8.0, OP.mult, -8.0, OP.add)
+        ts(v("t1"), v("n16", 0, 64), lo, OP.is_ge)
+        ts(v("t2"), v("n16", 0, 64), q, OP.is_le, 2 * BIG, OP.mult)
+        fill(v("rst%d" % k, 0, 64, w), -BIG)
+        ts(rw, rs, float(w), OP.add)
+        ts(v("ms%d" % k), v("i17"), rs, OP.not_equal)
+        tt(v("mq%d" % k), v("t1"), v("t2"), OP.mult)
+        ts(v("t3"), v("i17"), rw, OP.is_equal, SEP - 1.0, OP.mult)
+        ts(v("c%d" % k, 16, 68, 17), v("rtab"), bs, OP.mult, b8, OP.add)
+        ts(v("mq%d" % k), v("mq%d" % k), -BIG, OP.add)
+        tt(v("ms%d" % k), v("ms%d" % k), v("t3"), OP.add)
+        fill(v("ms%d" % k, 0, 68, 17), 0.0)
+
+    def early():
+        small(0)
+        fill(v("rst3"), BIG)
+        fill(v("rst3", 0, 64, 16), -BIG)
+        ts(v("md", 0, 64), v("n16", 0, 64), q, OP.is_gt)
+        ts(v("mda", 0, 64), v("n16", 0, 64), q1, OP.is_equal, DIG - 1.0, OP.mult)
+        tt(v("md", 0, 64), v("md", 0, 64), v("mda", 0, 64), OP.add)
+
+    def middle():
+        fill(v("rst4"), BIG)
+        fill(v("msk3"), 1.0)
+        fill(v("msk4"), 1.0)
+        ts(v("mh"), v("n16", 0, 64), q, OP.is_lt)
+        fill(v("rst4", 0, 64, 32), -BIG)
+        fill(v("msk3", 0, 68, 17), 0.0)
+        fill(v("msk4", 0, 132, 33), 0.0)
+        ts(v("mh", 15, 64, 16), v("n16", 15, 64, 16), q, OP.is_gt)
+        copy(v("c3", 16, 68, 34), v("rtab", 0, 4, 2))
+        ts(v("c3", 33, 68, 34), v("rtab", 1, 4, 2), -16.0, OP.add)
+        copy(v("c4", 32, 66, 33), v("rtab", 0, 2))
+        ts(v("c4", 98, 132, 33), v("rtab", 2, 4), -32.0, OP.add)
+        ts(v("mh"), v("mh"), 2 * BIG, OP.mult, -BIG, OP.add)
+
+    def later():
+        ts(m7, v("bff", 9, 10), 7.0, OP.is_equal)
+        ts(v("mda", 64, 512), v("n16", 64, 512), q1, OP.is_equal, DIG - 1.0, OP.mult)
+        ts(v("md", 64, 512), v("n16", 64, 512), q, OP.is_gt)
+        tt(v("md", 64, 512), v("md", 64, 512), v("mda", 64, 512), OP.add)
+        e5, e6, e7 = newcol(), newcol(), newcol()
+        ts(e5, v("bff", 4, 5), 2.0, OP.mult)
+        ts(e6, v("bff", 5, 6), 2.0, OP.mult, e5, OP.add)
+        ts(e7, v("bff", 6, 7), 16.0, OP.mult, e6, OP.add)
+        for k, w, e in ((5, 64, e5), (6, 128, e6), (7, 256, e7)):
+            ts(v("c%d" % k, w, 4 * w + 4, w + 1), v("rtab"), e, OP.add, sgn[k], OP.mult)
+        fill(v("ap6"), 0.0)
+        for r in range(R):
+            fill(v("list%d" % r), 0.0)
+        quant(v("vq"), v("vqs"), v("vt"))
+
+    def compact(c1, p0=0, p1=128):
+        return v("ds", 15, c1, 16, p0, p1)
+
+    for r in range(R):
+        lst = "list%d" % r
+        dg = T["dg%d" % r]
+        if r == 0:
+            copy(v("tb"), v("tbi"))
+            quant(v("xq", 0, 256), v("xqs", 0, 256), v("xt", 0, 1024))
+            quant(v("xq", 256, 512), v("xqs", 256, 512), v("xt", 1024, 2048))
+        else:
+            ts(v("tb"), v("tbf"), dsc, OP.mult)
+            quant(v("xq"), v("xqs"), v("xt"))
+        sgather(v("id0r"), v("iot"), v("tb"))
+
+        def score(k, bank, c0=0, c1=512):
+            mm(v(bank, 0, c1 - c0), v("uc", 128 * k, 128 * k + 128), v("ucs", 128 * k, 128 * k + 128), v("xq", c0, c1), v("xqs", c0, c1))
+
+        def unpack(b):
+            mm(v("b%d" % b), v("eq", 128 * b, 128 * b + 128), v("eqs", 128 * b, 128 * b + 128), v("xq"), v("xqs"))
+
+        score(0, "b4", 0, 256)
+        score(0, "b5", 256, 512)
+        if r == 0:
+            upick(1, 3)
+            early()
+        copy(v("sw0", 0, 256), v("b4", 0, 256))
+        act(v("sw0", 256, 512), v("b5", 0, 256))
+        vgather(v("g0"), v("sw0"), v("tb"))
+        score(1, "b6")
+        act(v("sw1"), v("b6"))
+        sgather(v("o1"), v("sw1"), v("tb"))
+        score(2, "b7")
+        act(v("sw2"), v("b7"))
+        if r == 0:
+            upick(3, 8)
+            for b in range(4):
+                quant(v("eq", 128 * b, 128 * b + 128), v("eqs", 128 * b, 128 * b + 128), v("ee", 512 * b, 512 * b + 512))
+        score(3, "b4")
+        unpack(0)
+        score(4, "b5")
+        unpack(1)
+        score(5, "b6")
+        unpack(2)
+        score(6, "b7")
+        unpack(3)
+
+        def tail(k, part):
+            dst = "idw" if k == 4 else "id%dr" % (k + 1)
+            if part == 0:
+                scatter(v(dst), v("rk"), v("id%dr" % k))
+            elif part == 1:
+                scan(v("ds", 0, 64), v("md", 0, 64), v(dst), 0.0, OP.mult, OP.add)
+            else:
+                if k < 3:
+                    ts(v("tbl%d" % k), compact(64), dsc, OP.mult)
+                    sgather(v("o%d" % (k + 2)), v("sw%d" % (k + 2)), v("tbl%d" % k))
+                act(v("lr", 4 * k, 4 * k + 4), compact(64))
+                dma("y", "dga%d%d" % (r, k), 1, ("dg%d" % r, 0, 128, k, k + 1, dg[k]), v("lr", 4 * k, 4 * k + 4))
+
+        for k in range(5):
+            w = 2 << k
+            G = v("g%d" % k)
+            C = "c%d" % k
+            scan(v("kk"), v("rst%d" % k), G, -BIG, OP.min, OP.max)
+            if k < 3:
+                tt(v("gm"), G, v("mq%d" % k), OP.min)
+            if k:
+                tail(k - 1, 0)
+            if k < 3:
+                scan(v("kd"), v("rst3"), v("gm"), -BIG, OP.min, OP.max)
+            else:
+                scan(v("kd"), v("kk"), v("mh"), BIG, OP.min, OP.max)
+            if k:
+                tail(k - 1, 1)
+            if k < 3:
+                ts(v("kds"), v("kd", 15, 64, 16), sgn[k], OP.mult)
+            else:
+                tt(v("kds"), v("kd", 14, 64, 16), v("kd", 15, 64, 16), OP.min)
+            if k:
+                tail(k - 1, 2)
+            if k < 3:
+                for c in range(4):
+                    ts(v(C, 17 * c, 17 * c + 16), v("kk", 16 * c, 16 * c + 16), sgn[k], OP.mult, v("kds", c, c + 1), OP.is_lt)
+                scan(v("sm", 0, 68), v("ms%d" % k), v(C), 0.0, OP.mult, OP.add)
+                ts(v("rk"), v("sm", 16, 68, 17), sgb[k], OP.mult)
+            else:
+                s = w + 1
+                for c in range(4):
+                    left = c % 2 == 0 if k == 3 else c < 2
+                    a = 16 * (c ^ 1) if k == 3 else 32 * left
+                    ts(v(C, s * c, s * c + w), v("kk", a, a + w), v("kds", c, c + 1), OP.is_lt if left else OP.is_le)
+                scan(v("sm", 0, 4 * s), v("msk%d" % k), v(C), 0.0, OP.mult, OP.add)
+                copy(v("rk"), v("sm", w, 4 * s, s))
+            if k < 4:
+                scatter(v("g%d" % (k + 1)), v("rk"), v("o%d" % (k + 1)))
+            if k == 0:
+                act(v("sw3"), v("b4"))
+                score(7, "b4")
+                act(v("fh0"), v("b0"), 0.5)
+            elif k < 3:
+                act(v("sw%d" % (k + 3)), v("b%d" % (k + 4)))
+                act(v("fh%d" % k), v("b%d" % k), 0.5)
+            elif k == 3:
+                act(v("sw6"), v("b7"))
+                act(v("sw7"), v("b4"))
+            if r == 0:
+                if k == 0:
+                    small(1)
+                elif k == 1:
+                    small(2)
+                    middle()
+                elif k == 2:
+                    later()
+        for j in range(3):
+            tail(4, j)
+
+        def merge(k, w, tab, ids, wname):
+            sgather(v("gg", w, 2 * w), v("sw%d" % k), v(tab, w // 16, w // 8))
+            vgather(v("gg", 0, w), v("sw%d" % k), v(tab, 0, w // 16))
+            scan(v("ko", 0, w), v("gg", 0, w), v("gg", 0, w), -BIG, OP.max, OP.max)
+            scan(v("kp", 0, w), v("gg", w, 2 * w), v("gg", w, 2 * w), -BIG, OP.max, OP.max)
+            if k == 5:
+                scan(v("hh"), v("ko", 0, 64), v("mh"), BIG, OP.min, OP.max)
+            else:
+                for a in range(4):
+                    c, p = 64 * (a % (w // 64)), (1, 32 * a, 32 * a + 32)
+                    scan(v("hh", 0, 64, *p), v("ko", c, c + 64, *p), v("mh", 0, 64, *p), BIG, OP.min, OP.max)
+            tt(v("kds"), v("hh", 14, 64, 16), v("hh", 15, 64, 16), OP.min)
+            ts(v("kds"), v("kds"), sgn[k], OP.mult)
+            s = w + 1
+            for c in range(4):
+                ts(v("c%d" % k, s * c, s * c + w), v("kp", 0, w), sgn[k], OP.mult, v("kds", c, c + 1), OP.is_lt)
+                accum(v("jk", 0, s), v("c%d" % k, s * c, s * c + s), v("sum4", c, c + 1))
+            ts(v("rk"), v("sum4"), sgn[k], OP.mult)
+            scatter(v(wname), v("rk"), v(ids))
+            scan(v("ds", 0, 2 * w), v("md", 0, 2 * w), v(wname), 0.0, OP.mult, OP.add)
+
+        def cross(n, out):
+            for a in range(4):
+                o, i = v("sh", 0, n, 1, 32 * a, 32 * a + 32), compact(16 * n, 32 * (a ^ 1), 32 * (a ^ 1) + 32)
+                if a < 2:
+                    copy(o, i)
+                else:
+                    act(o, i)
+            tt(out, compact(16 * n), v("sh", 0, n), OP.add)
+
+        def cross2(n, src, out):
+            copy(v("sh", 0, n, 1, 0, 64), v(src, 0, n, 1, 64, 128))
+            act(v("sh", 0, n, 1, 64, 128), v(src, 0, n, 1, 0, 64))
+            tt(out, v(src, 0, n), v("sh", 0, n), OP.add)
+
+        def owns(name, src, per):
+            for a in range(4):
+                c, p = 4 * (a % per), (1, 32 * a, 32 * a + 32)
+                ts(v(name, 0, 4, *p), v(src, c, c + 4, *p), dscp(32 * a, 32 * a + 32), OP.mult)
+
+        ts(v("tab5", 0, 4), compact(64), dsc, OP.mult)
+        for a in range(4):
+            o = 32 * (a ^ 1)
+            ts(v("tab5", 4, 8, 1, 32 * a, 32 * a + 32), compact(64, o, o + 32), dscp(o, o + 32), OP.mult)
+        merge(5, 64, "tab5", "idw", "w5%d" % r)
+        cross(8, v("a5"))
+        ts(v("tab6", 0, 8), v("a5"), dsc, OP.mult)
+        for a in range(2):
+            o = 64 * (1 - a)
+            ts(v("tab6", 8, 16, 1, 64 * a, 64 * a + 64), v("a5", 0, 8, 1, o, o + 64), dscp(o, o + 64), OP.mult)
+        owns("own6", "a5", 2)
+        sgather(v("id6"), v("iot"), v("own6"))
+        for B in range(4):
+            h = 16 * (4 * (B % 2) + B // 2)
+            dma("y", "dm%d" % r, 4, v(lst, 8 * B, 8 * B + 8, 1, 80, 96), v("a5", 0, 8, 1, h, h + 16))
+        for B in range(8):
+            h = 16 * group_of(B)
+            dma("y", "dl%d" % r, 8, v(lst, 4 * B, 4 * B + 4, 1, 0, 80), ("dg%d" % r, h, h + 16, 0, 5, dg[0:5, h:h + 16, :]))
+        merge(6, 128, "tab6", "id6", "w6%d" % r)
+        act(v("fh3"), v("b3"), 0.5)
+        cross(16, v("aa", 0, 16))
+        cross2(16, "aa", v("ap6", 0, 16))
+        trans(v("tr"), v("ap6"))
+        ts(v("tab7", 0, 16), v("ap6", 0, 16), dsc, OP.mult)
+        copy(v("sw", 0, 16), v("tr", 16, 32))
+        copy(v("sw", 16, 32), v("tr", 0, 16))
+        trans(v("tr2"), v("sw"))
+        ts(v("tab7", 16, 32), v("tr2", 0, 16), dsc, OP.mult)
+        owns("own7", "ap6", 4)
+        for j in range(2):
+            dma("y", "dn%d" % r, 2, v(lst, 16 * j, 16 * j + 16, 1, 96, 112), v("ap6", 0, 16, 1, 16 * j, 16 * j + 16))
+        sgather(v("id7"), v("iot"), v("own7"))
+        merge(7, 256, "tab7", "id7", "w7%d" % r)
+        cross(32, v("aa"))
+        cross2(32, "aa", v("l7"))
+        trans(v("tr"), v("l7"))
+        tt(v("sw", 0, 16), v("tr", 0, 16), v("tr", 16, 32), OP.add)
+        tt(v("sw", 16, 32), v("tr", 0, 16), v("tr", 16, 32), OP.add)
+        trans(v("tr7"), v("sw"))
+        ts(v("x7"), v("tr7"), m7, OP.mult)
+        tt(v("x7"), v("x7"), v(lst), OP.add)
+        ts(v("off"), v("x7"), dsc, OP.mult)
+        for b in range(4):
+            sgather(v("pa%d" % b), v("fh%d" % b), v("off", 0, 16))
+            ttg(v("zt", b, 1024, 4), v("fh%d" % b), v("off", 16, 32), v("pa%d" % b))
+        quant(v("zq"), v("zqs"), v("zt"))
+        rid, pid, _s = topo.addr(nxt)
+        eng = topo.engines(core, nxt)
+        for src, land, sem, loc, es in ((cd("zq"), cd("zl%d" % r), "ac%d" % r, "lc%d" % r, eng[0::2]),
+                                        (v("zqs"), v("zl%ds" % r), "as%d" % r, "ls%d" % r, eng[1::4])):
+            deps("g", [src], [])
+            g.remote_dma(land[5], src[5], T.sem[sem], T.sem[loc], pid, rid, sum(1 << e for e in es))
+            total[sem] = total[loc] = len(es)
+            note("g", (loc, len(es)), [src], [])
+            note("x", (sem, len(es)), [], [land])
+        if r < R - 1:
+            for B in range(8):
+                h = 16 * group_of(B)
+                dma("y", "db%d" % r, 8, v("tbf", 0, 4, 1, h, h + 16), v("tr7", 4 * B, 4 * B + 4, 1, 0, 16))
+        act(v("f0"), v("b0"))
+        act(v("f1"), v("b1"))
+        scatter(v("posw"), v("off"), v("iotm"))
+        scan(v("pds"), v("md"), v("posw"), 0.0, OP.mult, OP.add)
+        ts(v("pos"), v("pds", 15, 512, 16), dsc, OP.mult)
+        if r == R - 1:
+            sgather(v("row"), v("iot"), v("off"))
+            dma("y", "dod", 1, ("od", 0, 8, 0, 512, T.od[:, :]), ("row", 0, 128, 0, 512, T.row[0:128:16, :]))
+        for b in range(4):
+            mm(v("b%d" % (4 + b), 0, 256), v("wq", 128 * b, 128 * b + 128), v("wqs", 128 * b, 128 * b + 128), v("zl%d" % r), v("zl%ds" % r))
+        ts(v("pp0"), v("b4", 0, 256), 0.03125, OP.mult)
+        act(v("pp1"), v("b5", 0, 256), 0.03125)
+        act(v("pp2"), v("b6", 0, 256), 0.03125)
+        sgather(v("gp2"), v("pp2"), v("pos"))
+        act(v("pp3"), v("b7", 0, 256), 0.03125)
+        sgather(v("gp3"), v("pp3"), v("pos"))
+        for b in range(2):
+            ttg(v("xt", b, 2048, 4), v("pp%d" % b), v("pos"), v("f%d" % b))
+        for b in range(2, 4):
+            tt(v("xt", b, 2048, 4), v("gp%d" % b), v("b%d" % b), OP.add)
+
+    quant(v("xq"), v("xqs"), v("xt"))
+    mm(v("b4"), v("vq"), v("vqs"), v("xq"), v("xqs"))
+    dma("y", "doc", 1, ("oc", 0, 128, 0, 2048, T.oc[:, :]), cd("xq"))
+    for k in range(4):
+        dma("y", "dos", 4, ("osc", 4 * k, 4 * k + 4, 0, 512, T.osc[4 * k:4 * k + 4, :]), v("xqs", 0, 512, 1, 32 * k, 32 * k + 4))
+    act(v("yy"), v("b4"))
+    dma("y", "dy", 1, ("y", 0, 128, 0, 512, T.y[:, :]), v("yy"))
+    for k in semof:
+        need("g", (semof[k], count[k]))
+    for s in total:
+        need("g", (s, total[s]))

@@ -1,6 +1,7 @@
 from concourse.mybir import dt, AluOpType as OP, ActivationFunctionType as AF
 
 BIG = 2.0 ** 75
+EPS = 2.0 ** -120
 SEP = 64.0
 DIG = 2.0 ** 14
 R = 3
@@ -21,25 +22,27 @@ def _part(name, cols, arena="ar"):
     _used[arena] += -(-cols // 16) * 16
 
 
-for _n, _c in (("n16", 512), ("i17", 68), ("iot", 512), ("iotm", 512), ("io4", 4), ("bff", 16), ("sg", 6), ("sgk", 24), ("rtab", 4),
-               ("mh", 64), ("md", 512), ("mda", 512), ("t1", 64), ("t2", 64), ("t3", 68), ("msk3", 68), ("msk4", 132),
+for _n, _c in (("n16", 512), ("i17", 68), ("iot", 512), ("iotm", 512), ("io4", 4), ("bff", 16), ("sgk", 32), ("rtab", 4),
+               ("mh", 64), ("md", 512), ("mda", 512), ("t2", 64), ("msk3", 68), ("msk4", 132), ("msk5", 260),
                ("c0", 68), ("c1", 68), ("c2", 68), ("c3", 68), ("c4", 132), ("c5", 260), ("c6", 516), ("c7", 1028),
-               ("kk", 64), ("gm", 64), ("kd", 64), ("kds", 4), ("sm", 132), ("ko", 256), ("kp", 256), ("gg", 512), ("hh", 64),
-               ("jk", 260), ("sum4", 4), ("sh", 32), ("aa", 32), ("a5", 8), ("ap6", 32), ("tr", 32), ("sw", 32), ("tr2", 32), ("tr7", 32), ("x7", 32), ("l7", 32),
+               ("kk", 64), ("gm", 64), ("kd", 64), ("sm", 260), ("no", 256), ("np", 256), ("gg", 512), ("hh", 64), ("g5", 64), ("g6", 128), ("o5", 64), ("o6", 64),
+               ("jk", 1028), ("sum4", 4), ("sh", 32), ("shs", 128), ("aa", 32), ("a5", 8), ("ap6", 32), ("tr", 32), ("sw", 32), ("tr2", 32),
+               ("qa", 32), ("qb", 32), ("qt", 32), ("qe", 32), ("tl", 32), ("tr7", 32),
                ("id6", 64), ("id7", 64), ("posw", 512), ("pds", 512), ("lr", 20), ("tbf", 4), ("idw", 64), ("ds", 512)):
     _part(_n, _c)
 for _g in range(5):
     for _s in ("g%d", "o%d", "id%dr", "rst%d"):
-        _part(_s % _g, 64)
+        if _s != "o%d" or _g:
+            _part(_s % _g, 64)
 for _g in range(3):
-    _part("mq%d" % _g, 64)
-    _part("ms%d" % _g, 68)
+    for _s, _c in (("mq%d", 64), ("ms%d", 68), ("t1%d", 64), ("t3%d", 68)):
+        _part(_s % _g, _c)
 for _r in range(R):
     _part("list%d" % _r, 32)
-    for _g, _c in ((5, 128), (6, 256), (7, 512)):
-        _part("w%d%d" % (_g, _r), _c)
+    for _s, _c in (("w5s%d", 128), ("w5%d", 128), ("w6%d", 256), ("w7%d", 512)):
+        _part(_s % _r, _c)
     SCRATCH["dg%d" % _r] = ("dram", [5, 128, 4], "float32")
-for _n, _c in (("uo", 64), ("rk", 4), ("tb", 4), ("tab5", 8), ("tab6", 16), ("tab7", 32), ("own6", 4), ("own7", 4), ("off", 32), ("pos", 32),
+for _n, _c in (("uo", 64), ("rk", 4), ("tb", 4), ("tab5", 4), ("tab7", 32), ("own6", 4), ("own7", 4), ("off", 32), ("pos", 32),
                ("tbl0", 4), ("tbl1", 4), ("tbl2", 4), ("tbl3", 4)):
     _part(_n, _c, "ar16")
 _buf("ar", _used["ar"])
@@ -92,6 +95,9 @@ def rank_program(g, core, T, topo):
         c0, c1 = c0 + at, (cols if c1 is None else c1) + at
         ap = T[name][p0:p1, c0:c1] if st == 1 else T[name][p0:p1, c0:c1:st]
         return (name, p0, p1, c0, c1, ap)
+
+    def quad(name, c0, c1, a):
+        return v(name, c0, c1, 1, 32 * a, 32 * a + 32)
 
     def deps(q, ins, outs):
         toks = {}
@@ -197,117 +203,105 @@ def rank_program(g, core, T, topo):
     dma("y", "dw", 2, cd("wq"), ("wc", 0, 128, 0, 2048, T.wc[:, :]))
     dma("y", "dw", 2, v("wqs"), ("ws", 0, 128, 0, 512, T.ws[:, :]))
 
-    iota(v("uoi"), [[16, 8], [0, 8]])
     iota(v("pi"), [[0, 1]], 0, 1)
     iota(v("n16", 0, 64), [[0, 4], [1, 16]])
     iota(v("io4"), [[16, 4]])
     iota(v("i17"), [[0, 4], [1, 17]])
+    iota(v("uoi"), [[16, 8], [0, 8]])
     iota(v("iot"), [[1, 512]])
     fill(v("ones"), 1.0)
     for b in range(4):
         o, i = v("ee", 512 * b, 512 * b + 512), v("ones")
         op("g", lambda e: e.affine_select(o[5], i[5], [[-1, 512]], OP.is_equal, 0.0, b, 4), [o], [i])
     iota(v("n16", 64, 512), [[0, 28], [1, 16]])
+    iota(v("ap6"), [[0, 32]])
     for r in range(R):
-        for k, c in ((5, 128), (6, 256), (7, 512)):
-            iota(v("w%d%d" % (k, r)), [[0, c]])
+        for n, c in (("w5s%d", 128), ("w5%d", 128), ("w6%d", 256), ("w7%d", 512), ("list%d", 32)):
+            iota(v(n % r), [[0, c]])
     iota(v("iotm"), [[0, 2], [1, 256]])
-
-    copy(v("uo"), v("uoi"))
-    for j, m in enumerate((15, 2, 4, 8, 32, 64, 16, 14, 12)):
-        ts(v("bi", j, j + 1), v("pi"), m, OP.bitwise_and)
-    ts(v("bi", 9, 10), v("pi"), 4, OP.arith_shift_right)
-    copy(v("bff", 0, 10), v("bi", 0, 10))
-    q = v("bff", 0, 1)
-    quant(v("uq"), v("uqs"), v("ut"))
 
     def upick(a, b):
         o, w, f = v("uc", 128 * a, 128 * b), v("uq"), v("uo", 8 * a, 8 * b)
         op("v", lambda e: e.tensor_copy(o[5].bitcast(dt.uint32), w[5].bitcast(dt.uint32).indirect(f[5])), [o], [w, f])
         sgather(v("ucs", 128 * a, 128 * b), v("uqs"), f)
 
-    upick(0, 1)
-    sgn = {}
-    for i, (k, c, m) in enumerate(((0, 1, 2), (1, 2, 4), (2, 3, 8), (5, 4, 32), (6, 5, 64), (7, 6, 16))):
-        sgn[k] = v("sg", i, i + 1)
-        ts(sgn[k], v("bff", c, c + 1), -2.0 / m, OP.mult, 1.0, OP.add)
+    WID = {0: 2, 1: 4, 2: 8, 3: 16, 4: 32}
+    for k in range(5):
+        fill(v("rst%d" % k), -BIG)
+    for n in ("msk3", "msk4", "msk5"):
+        fill(v(n), 1.0)
+    for j, m in enumerate((15, 2, 4, 8, 32, 64, 16, 14, 12)):
+        ts(v("bi", j, j + 1), v("pi"), m, OP.bitwise_and)
+    for k, w in WID.items():
+        fill(v("rst%d" % k, 0, 64, w), BIG)
+    fill(v("msk3", 0, 68, 17), 0.0)
+    fill(v("msk4", 0, 132, 33), 0.0)
+    fill(v("msk5", 0, 260, 65), 0.0)
+    copy(v("bff", 0, 9), v("bi", 0, 9))
+    copy(v("uo"), v("uoi"))
+    q = v("bff", 0, 1)
     col = [0]
 
     def newcol():
         col[0] += 1
         return v("sgk", col[0] - 1, col[0])
 
-    dsc, m7, q1 = newcol(), newcol(), newcol()
+    dsc, q1, e6, e7 = newcol(), newcol(), newcol(), newcol()
 
     def dscp(a, b):
         return v("sgk", 0, 1, 1, a, b)
 
+    bit, th, rs0, rs, rw = {}, {}, {}, {}, {}
     ts(dsc, q, 15.0, OP.is_equal, 1.0 - 1.0 / DIG, OP.mult)
     ts(q1, q, 1.0, OP.add)
     ts(v("rtab"), v("io4"), q, OP.add)
+    for k, c, m in ((0, 1, 2), (1, 2, 4), (2, 3, 8), (5, 4, 32), (6, 5, 64), (7, 6, 16)):
+        bit[k], th[k] = v("bff", c, c + 1), newcol()
+        ts(th[k], bit[k], -EPS / m, OP.mult)
+    lo = {0: v("bff", 7, 8), 1: v("bff", 8, 9), 2: bit[2]}
+    for k in range(3):
+        rs0[k], rs[k], rw[k] = newcol(), newcol(), newcol()
+        ts(rs0[k], bit[k], -2.0, OP.mult, lo[k], OP.add)
+        ts(v("t1%d" % k), v("n16", 0, 64), lo[k], OP.is_ge)
+    ts(v("t2"), v("n16", 0, 64), q, OP.is_le, -2 * BIG, OP.mult)
+    ts(v("mh"), v("n16", 0, 64), q, OP.is_equal, -2 * BIG, OP.mult)
+    ts(v("md", 0, 64), v("n16", 0, 64), q, OP.is_gt)
+    ts(e6, bit[5], 2.0, OP.mult)
     ts(dsc, dsc, 1.0 / DIG, OP.add)
-    sgb = {}
+    for k in range(3):
+        ts(rs[k], rs0[k], float(WID[k]), OP.add)
+        ts(rw[k], rs0[k], 2.0 * WID[k], OP.add)
+        tt(v("mq%d" % k), v("t1%d" % k), v("t2"), OP.mult)
+        ts(v("c%d" % k, 16, 68, 17), v("rtab"), bit[k], OP.subtract, SEP, OP.mult)
+    ts(v("mda", 0, 64), v("n16", 0, 64), q1, OP.is_equal, DIG - 1.0, OP.mult)
+    ts(v("mh"), v("mh"), BIG, OP.add)
+    for k in range(3):
+        ts(v("mq%d" % k), v("mq%d" % k), BIG, OP.add)
+        ts(v("ms%d" % k), v("i17"), rs[k], OP.not_equal)
+        ts(v("t3%d" % k), v("i17"), rw[k], OP.is_equal, SEP - 1.0, OP.mult)
+    tt(v("md", 0, 64), v("md", 0, 64), v("mda", 0, 64), OP.add)
+    for k in range(3):
+        tt(v("ms%d" % k), v("ms%d" % k), v("t3%d" % k), OP.add)
+    quant(v("uq"), v("uqs"), v("ut"))
+    upick(0, 1)
 
-    def small(k):
-        w = 2 << k
-        fill(v("rst%d" % k), BIG)
-        lo = v("bff", (7, 8, 3)[k], (7, 8, 3)[k] + 1)
-        rs, rw, bs, b8 = newcol(), newcol(), newcol(), newcol()
-        sgb[k] = newcol()
-        ts(sgb[k], sgn[k], 1.0 / SEP, OP.mult)
-        ts(rs, sgn[k], float(w), OP.mult, lo, OP.add)
-        ts(bs, sgn[k], SEP, OP.mult)
-        ts(b8, sgn[k], 8.0, OP.mult, -8.0, OP.add)
-        ts(v("t1"), v("n16", 0, 64), lo, OP.is_ge)
-        ts(v("t2"), v("n16", 0, 64), q, OP.is_le, 2 * BIG, OP.mult)
-        fill(v("rst%d" % k, 0, 64, w), -BIG)
-        ts(rw, rs, float(w), OP.add)
-        ts(v("ms%d" % k), v("i17"), rs, OP.not_equal)
-        tt(v("mq%d" % k), v("t1"), v("t2"), OP.mult)
-        ts(v("t3"), v("i17"), rw, OP.is_equal, SEP - 1.0, OP.mult)
-        ts(v("c%d" % k, 16, 68, 17), v("rtab"), bs, OP.mult, b8, OP.add)
-        ts(v("mq%d" % k), v("mq%d" % k), -BIG, OP.add)
-        tt(v("ms%d" % k), v("ms%d" % k), v("t3"), OP.add)
-        fill(v("ms%d" % k, 0, 68, 17), 0.0)
-
-    def early():
-        small(0)
-        fill(v("rst3"), BIG)
-        fill(v("rst3", 0, 64, 16), -BIG)
-        ts(v("md", 0, 64), v("n16", 0, 64), q, OP.is_gt)
-        ts(v("mda", 0, 64), v("n16", 0, 64), q1, OP.is_equal, DIG - 1.0, OP.mult)
-        tt(v("md", 0, 64), v("md", 0, 64), v("mda", 0, 64), OP.add)
-
-    def middle():
-        fill(v("rst4"), BIG)
-        fill(v("msk3"), 1.0)
-        fill(v("msk4"), 1.0)
-        ts(v("mh"), v("n16", 0, 64), q, OP.is_lt)
-        fill(v("rst4", 0, 64, 32), -BIG)
-        fill(v("msk3", 0, 68, 17), 0.0)
-        fill(v("msk4", 0, 132, 33), 0.0)
-        ts(v("mh", 15, 64, 16), v("n16", 15, 64, 16), q, OP.is_gt)
+    def rest():
+        for k in range(3):
+            fill(v("ms%d" % k, 0, 68, 17), 0.0)
         copy(v("c3", 16, 68, 34), v("rtab", 0, 4, 2))
         ts(v("c3", 33, 68, 34), v("rtab", 1, 4, 2), -16.0, OP.add)
         copy(v("c4", 32, 66, 33), v("rtab", 0, 2))
         ts(v("c4", 98, 132, 33), v("rtab", 2, 4), -32.0, OP.add)
-        ts(v("mh"), v("mh"), 2 * BIG, OP.mult, -BIG, OP.add)
+        ts(e7, bit[6], 2.0, OP.mult, e6, OP.add)
+        copy(v("c5", 64, 260, 65), v("rtab"))
+        ts(v("c6", 128, 516, 129), v("rtab"), e6, OP.add)
+        ts(v("c7", 256, 1028, 257), v("rtab"), e7, OP.add)
 
-    def later():
-        ts(m7, v("bff", 9, 10), 7.0, OP.is_equal)
+    def wide():
         ts(v("mda", 64, 512), v("n16", 64, 512), q1, OP.is_equal, DIG - 1.0, OP.mult)
         ts(v("md", 64, 512), v("n16", 64, 512), q, OP.is_gt)
-        tt(v("md", 64, 512), v("md", 64, 512), v("mda", 64, 512), OP.add)
-        e5, e6, e7 = newcol(), newcol(), newcol()
-        ts(e5, v("bff", 4, 5), 2.0, OP.mult)
-        ts(e6, v("bff", 5, 6), 2.0, OP.mult, e5, OP.add)
-        ts(e7, v("bff", 6, 7), 16.0, OP.mult, e6, OP.add)
-        for k, w, e in ((5, 64, e5), (6, 128, e6), (7, 256, e7)):
-            ts(v("c%d" % k, w, 4 * w + 4, w + 1), v("rtab"), e, OP.add, sgn[k], OP.mult)
-        fill(v("ap6"), 0.0)
-        for r in range(R):
-            fill(v("list%d" % r), 0.0)
         quant(v("vq"), v("vqs"), v("vt"))
+        tt(v("md", 64, 512), v("md", 64, 512), v("mda", 64, 512), OP.add)
 
     def compact(c1, p0=0, p1=128):
         return v("ds", 15, c1, 16, p0, p1)
@@ -317,11 +311,10 @@ def rank_program(g, core, T, topo):
         dg = T["dg%d" % r]
         if r == 0:
             copy(v("tb"), v("tbi"))
-            quant(v("xq", 0, 256), v("xqs", 0, 256), v("xt", 0, 1024))
-            quant(v("xq", 256, 512), v("xqs", 256, 512), v("xt", 1024, 2048))
         else:
             ts(v("tb"), v("tbf"), dsc, OP.mult)
-            quant(v("xq"), v("xqs"), v("xt"))
+        quant(v("xq", 0, 256), v("xqs", 0, 256), v("xt", 0, 1024))
+        quant(v("xq", 256, 512), v("xqs", 256, 512), v("xt", 1024, 2048))
         sgather(v("id0r"), v("iot"), v("tb"))
 
         def score(k, bank, c0=0, c1=512):
@@ -333,21 +326,23 @@ def rank_program(g, core, T, topo):
         score(0, "b4", 0, 256)
         score(0, "b5", 256, 512)
         if r == 0:
-            upick(1, 3)
-            early()
-        copy(v("sw0", 0, 256), v("b4", 0, 256))
-        act(v("sw0", 256, 512), v("b5", 0, 256))
+            upick(1, 2)
+        ts(v("sw0", 0, 256), v("b4", 0, 256), -1.0, OP.mult)
+        act(v("sw0", 256, 512), v("b5", 0, 256), -1.0)
+        if r == 0:
+            rest()
         vgather(v("g0"), v("sw0"), v("tb"))
         score(1, "b6")
-        act(v("sw1"), v("b6"))
+        act(v("sw1"), v("b6"), -1.0)
         sgather(v("o1"), v("sw1"), v("tb"))
-        score(2, "b7")
-        act(v("sw2"), v("b7"))
         if r == 0:
-            upick(3, 8)
+            upick(2, 8)
+        score(2, "b7")
+        act(v("sw2"), v("b7"), -1.0)
+        score(3, "b4")
+        if r == 0:
             for b in range(4):
                 quant(v("eq", 128 * b, 128 * b + 128), v("eqs", 128 * b, 128 * b + 128), v("ee", 512 * b, 512 * b + 512))
-        score(3, "b4")
         unpack(0)
         score(4, "b5")
         unpack(1)
@@ -363,9 +358,9 @@ def rank_program(g, core, T, topo):
             elif part == 1:
                 scan(v("ds", 0, 64), v("md", 0, 64), v(dst), 0.0, OP.mult, OP.add)
             else:
-                if k < 3:
-                    ts(v("tbl%d" % k), compact(64), dsc, OP.mult)
-                    sgather(v("o%d" % (k + 2)), v("sw%d" % (k + 2)), v("tbl%d" % k))
+                tab = "tab5" if k == 4 else "tbl%d" % k
+                ts(v(tab), compact(64), dsc, OP.mult)
+                sgather(v("o%d" % (k + 2)), v("sw%d" % (k + 2)), v(tab))
                 act(v("lr", 4 * k, 4 * k + 4), compact(64))
                 dma("y", "dga%d%d" % (r, k), 1, ("dg%d" % r, 0, 128, k, k + 1, dg[k]), v("lr", 4 * k, 4 * k + 4))
 
@@ -373,143 +368,158 @@ def rank_program(g, core, T, topo):
             w = 2 << k
             G = v("g%d" % k)
             C = "c%d" % k
-            scan(v("kk"), v("rst%d" % k), G, -BIG, OP.min, OP.max)
             if k < 3:
-                tt(v("gm"), G, v("mq%d" % k), OP.min)
-            if k:
-                tail(k - 1, 0)
-            if k < 3:
-                scan(v("kd"), v("rst3"), v("gm"), -BIG, OP.min, OP.max)
+                tt(v("gm"), G, v("mq%d" % k), OP.max)
+                scan(v("kk"), v("rst%d" % k), G, BIG, OP.max, OP.min)
+                if k:
+                    tail(k - 1, 0)
+                scan(v("kd"), v("rst3"), v("gm"), BIG, OP.max, OP.min)
             else:
-                scan(v("kd"), v("kk"), v("mh"), BIG, OP.min, OP.max)
+                scan(v("kk"), v("rst%d" % k), G, BIG, OP.max, OP.min)
+                tail(k - 1, 0)
+                scan(v("kd"), v("mh"), v("kk"), BIG, OP.min, OP.max)
             if k:
                 tail(k - 1, 1)
-            if k < 3:
-                ts(v("kds"), v("kd", 15, 64, 16), sgn[k], OP.mult)
-            else:
-                tt(v("kds"), v("kd", 14, 64, 16), v("kd", 15, 64, 16), OP.min)
+            s = 17 if k < 3 else w + 1
+            for c in range(4):
+                x = v("kd", 16 * c + 15, 16 * c + 16)
+                if k < 3:
+                    ts(v(C, s * c, s * c + 16), v("kk", 16 * c, 16 * c + 16), x, OP.subtract, th[k], OP.is_gt)
+                else:
+                    left = c % 2 == 0 if k == 3 else c < 2
+                    a = 16 * (c ^ 1) if k == 3 else 32 * left
+                    ts(v(C, s * c, s * c + w), v("kk", a, a + w), x, OP.is_gt if left else OP.is_ge)
+            scan(v("sm", 0, 4 * s), v(("ms%d" if k < 3 else "msk%d") % k), v(C), 0.0, OP.mult, OP.add)
             if k:
                 tail(k - 1, 2)
             if k < 3:
-                for c in range(4):
-                    ts(v(C, 17 * c, 17 * c + 16), v("kk", 16 * c, 16 * c + 16), sgn[k], OP.mult, v("kds", c, c + 1), OP.is_lt)
-                scan(v("sm", 0, 68), v("ms%d" % k), v(C), 0.0, OP.mult, OP.add)
-                ts(v("rk"), v("sm", 16, 68, 17), sgb[k], OP.mult)
+                ts(v("rk"), v("sm", 16, 68, 17), 1.0 / SEP, OP.mult)
             else:
-                s = w + 1
-                for c in range(4):
-                    left = c % 2 == 0 if k == 3 else c < 2
-                    a = 16 * (c ^ 1) if k == 3 else 32 * left
-                    ts(v(C, s * c, s * c + w), v("kk", a, a + w), v("kds", c, c + 1), OP.is_lt if left else OP.is_le)
-                scan(v("sm", 0, 4 * s), v("msk%d" % k), v(C), 0.0, OP.mult, OP.add)
                 copy(v("rk"), v("sm", w, 4 * s, s))
-            if k < 4:
-                scatter(v("g%d" % (k + 1)), v("rk"), v("o%d" % (k + 1)))
+            scatter(v("g%d" % (k + 1)), v("rk"), v("o%d" % (k + 1)))
             if k == 0:
-                act(v("sw3"), v("b4"))
+                act(v("sw3"), v("b4"), -1.0)
                 score(7, "b4")
                 act(v("fh0"), v("b0"), 0.5)
             elif k < 3:
-                act(v("sw%d" % (k + 3)), v("b%d" % (k + 4)))
+                act(v("sw%d" % (k + 3)), v("b%d" % (k + 4)), -1.0)
                 act(v("fh%d" % k), v("b%d" % k), 0.5)
             elif k == 3:
-                act(v("sw6"), v("b7"))
-                act(v("sw7"), v("b4"))
-            if r == 0:
-                if k == 0:
-                    small(1)
-                elif k == 1:
-                    small(2)
-                    middle()
-                elif k == 2:
-                    later()
-        for j in range(3):
-            tail(4, j)
+                act(v("sw6"), v("b7"), -1.0)
+                act(v("sw7"), v("b4"), -1.0)
+            if r == 0 and k == 1:
+                wide()
 
-        def merge(k, w, tab, ids, wname):
-            sgather(v("gg", w, 2 * w), v("sw%d" % k), v(tab, w // 16, w // 8))
-            vgather(v("gg", 0, w), v("sw%d" % k), v(tab, 0, w // 16))
-            scan(v("ko", 0, w), v("gg", 0, w), v("gg", 0, w), -BIG, OP.max, OP.max)
-            scan(v("kp", 0, w), v("gg", w, 2 * w), v("gg", w, 2 * w), -BIG, OP.max, OP.max)
-            if k == 5:
-                scan(v("hh"), v("ko", 0, 64), v("mh"), BIG, OP.min, OP.max)
+        def runmin(out, in_):
+            scan(out, in_, in_, BIG, OP.min, OP.min)
+
+        def hold(w):
+            if w == 64:
+                scan(v("hh"), v("mh"), v("no", 0, 64), BIG, OP.min, OP.max)
             else:
                 for a in range(4):
-                    c, p = 64 * (a % (w // 64)), (1, 32 * a, 32 * a + 32)
-                    scan(v("hh", 0, 64, *p), v("ko", c, c + 64, *p), v("mh", 0, 64, *p), BIG, OP.min, OP.max)
-            tt(v("kds"), v("hh", 14, 64, 16), v("hh", 15, 64, 16), OP.min)
-            ts(v("kds"), v("kds"), sgn[k], OP.mult)
-            s = w + 1
-            for c in range(4):
-                ts(v("c%d" % k, s * c, s * c + w), v("kp", 0, w), sgn[k], OP.mult, v("kds", c, c + 1), OP.is_lt)
-                accum(v("jk", 0, s), v("c%d" % k, s * c, s * c + s), v("sum4", c, c + 1))
-            ts(v("rk"), v("sum4"), sgn[k], OP.mult)
-            scatter(v(wname), v("rk"), v(ids))
-            scan(v("ds", 0, 2 * w), v("md", 0, 2 * w), v(wname), 0.0, OP.mult, OP.add)
+                    c = 64 * (a % (w // 64))
+                    scan(quad("hh", 0, 64, a), quad("mh", 0, 64, a), quad("no", c, c + 64, a), BIG, OP.min, OP.max)
 
-        def cross(n, out):
+        def versus(k, w, c):
+            s = w + 1
+            ts(v("c%d" % k, s * c, s * c + w), v("np", 0, w), v("hh", 16 * c + 15, 16 * c + 16), OP.subtract, th[k], OP.is_gt)
+            if k > 5:
+                accum(v("jk", s * c, s * c + s), v("c%d" % k, s * c, s * c + s), v("sum4", c, c + 1))
+
+        def swap1(out, in_, n, src=quad):
             for a in range(4):
-                o, i = v("sh", 0, n, 1, 32 * a, 32 * a + 32), compact(16 * n, 32 * (a ^ 1), 32 * (a ^ 1) + 32)
+                o, i = quad(out, 0, n, a), src(in_, 0, n, a ^ 1)
                 if a < 2:
                     copy(o, i)
                 else:
                     act(o, i)
-            tt(out, compact(16 * n), v("sh", 0, n), OP.add)
 
-        def cross2(n, src, out):
-            copy(v("sh", 0, n, 1, 0, 64), v(src, 0, n, 1, 64, 128))
-            act(v("sh", 0, n, 1, 64, 128), v(src, 0, n, 1, 0, 64))
-            tt(out, v(src, 0, n), v("sh", 0, n), OP.add)
+        def dsq(_n, c0, n, a):
+            return compact(16 * n, 32 * a, 32 * a + 32)
+
+        def swap2(out, in_, n):
+            copy(v(out, 0, n, 1, 0, 64), v(in_, 0, n, 1, 64, 128))
+            act(v(out, 0, n, 1, 64, 128), v(in_, 0, n, 1, 0, 64))
 
         def owns(name, src, per):
             for a in range(4):
-                c, p = 4 * (a % per), (1, 32 * a, 32 * a + 32)
-                ts(v(name, 0, 4, *p), v(src, c, c + 4, *p), dscp(32 * a, 32 * a + 32), OP.mult)
+                c = 4 * (a % per)
+                ts(quad(name, 0, 4, a), quad(src, c, c + 4, a), dscp(32 * a, 32 * a + 32), OP.mult)
 
-        ts(v("tab5", 0, 4), compact(64), dsc, OP.mult)
-        for a in range(4):
-            o = 32 * (a ^ 1)
-            ts(v("tab5", 4, 8, 1, 32 * a, 32 * a + 32), compact(64, o, o + 32), dscp(o, o + 32), OP.mult)
-        merge(5, 64, "tab5", "idw", "w5%d" % r)
-        cross(8, v("a5"))
-        ts(v("tab6", 0, 8), v("a5"), dsc, OP.mult)
-        for a in range(2):
-            o = 64 * (1 - a)
-            ts(v("tab6", 8, 16, 1, 64 * a, 64 * a + 64), v("a5", 0, 8, 1, o, o + 64), dscp(o, o + 64), OP.mult)
+        runmin(v("no", 0, 64), v("g5"))
+        tail(4, 0)
+        swap1("np", "no", 64)
+        hold(64)
+        tail(4, 1)
+        for c in range(4):
+            versus(5, 64, c)
+        tail(4, 2)
+        scan(v("sm"), v("msk5"), v("c5"), 0.0, OP.mult, OP.add)
+        copy(v("rk"), v("sm", 64, 260, 65))
+        scatter(v("w5s%d" % r), v("rk"), v("o6"))
+        swap1("shs", "w5s%d" % r, 128)
+        scatter(v("w5%d" % r), v("rk"), v("idw"))
+        tt(v("g6"), v("w5s%d" % r), v("shs"), OP.add)
+        scan(v("ds", 0, 128), v("md", 0, 128), v("w5%d" % r), 0.0, OP.mult, OP.add)
+        runmin(v("no", 0, 128), v("g6"))
+        swap2("np", "no", 128)
+        hold(128)
+        swap1("sh", "ds", 8, dsq)
+        versus(6, 128, 0)
+        versus(6, 128, 1)
+        tt(v("a5"), compact(128), v("sh", 0, 8), OP.add)
+        versus(6, 128, 2)
+        versus(6, 128, 3)
         owns("own6", "a5", 2)
         sgather(v("id6"), v("iot"), v("own6"))
+        ts(v("rk"), v("sum4"), 1.0, OP.mult)
+        scatter(v("w6%d" % r), v("rk"), v("id6"))
         for B in range(4):
             h = 16 * (4 * (B % 2) + B // 2)
             dma("y", "dm%d" % r, 4, v(lst, 8 * B, 8 * B + 8, 1, 80, 96), v("a5", 0, 8, 1, h, h + 16))
         for B in range(8):
             h = 16 * group_of(B)
             dma("y", "dl%d" % r, 8, v(lst, 4 * B, 4 * B + 4, 1, 0, 80), ("dg%d" % r, h, h + 16, 0, 5, dg[0:5, h:h + 16, :]))
-        merge(6, 128, "tab6", "id6", "w6%d" % r)
-        act(v("fh3"), v("b3"), 0.5)
-        cross(16, v("aa", 0, 16))
-        cross2(16, "aa", v("ap6", 0, 16))
+        scan(v("ds", 0, 256), v("md", 0, 256), v("w6%d" % r), 0.0, OP.mult, OP.add)
+        swap1("sh", "ds", 16, dsq)
+        tt(v("aa", 0, 16), compact(256), v("sh", 0, 16), OP.add)
+        swap2("sh", "aa", 16)
+        tt(v("ap6", 0, 16), v("aa", 0, 16), v("sh", 0, 16), OP.add)
         trans(v("tr"), v("ap6"))
         ts(v("tab7", 0, 16), v("ap6", 0, 16), dsc, OP.mult)
         copy(v("sw", 0, 16), v("tr", 16, 32))
         copy(v("sw", 16, 32), v("tr", 0, 16))
         trans(v("tr2"), v("sw"))
-        ts(v("tab7", 16, 32), v("tr2", 0, 16), dsc, OP.mult)
         owns("own7", "ap6", 4)
+        ts(v("tab7", 16, 32), v("tr2", 0, 16), dsc, OP.mult)
         for j in range(2):
             dma("y", "dn%d" % r, 2, v(lst, 16 * j, 16 * j + 16, 1, 96, 112), v("ap6", 0, 16, 1, 16 * j, 16 * j + 16))
+        sgather(v("gg", 256, 512), v("sw7"), v("tab7", 16, 32))
+        vgather(v("gg", 0, 256), v("sw7"), v("tab7", 0, 16))
         sgather(v("id7"), v("iot"), v("own7"))
-        merge(7, 256, "tab7", "id7", "w7%d" % r)
-        cross(32, v("aa"))
-        cross2(32, "aa", v("l7"))
-        trans(v("tr"), v("l7"))
-        tt(v("sw", 0, 16), v("tr", 0, 16), v("tr", 16, 32), OP.add)
-        tt(v("sw", 16, 32), v("tr", 0, 16), v("tr", 16, 32), OP.add)
-        trans(v("tr7"), v("sw"))
-        ts(v("x7"), v("tr7"), m7, OP.mult)
-        tt(v("x7"), v("x7"), v(lst), OP.add)
-        ts(v("off"), v("x7"), dsc, OP.mult)
-        for b in range(4):
+        runmin(v("no"), v("gg", 0, 256))
+        runmin(v("np"), v("gg", 256, 512))
+        hold(256)
+        for c in range(4):
+            versus(7, 256, c)
+        act(v("fh3"), v("b3"), 0.5)
+        ts(v("rk"), v("sum4"), 1.0, OP.mult)
+        scatter(v("w7%d" % r), v("rk"), v("id7"))
+        ts(v("off", 0, 32, 1, 0, 96), v(lst, 0, 32, 1, 0, 96), dscp(0, 96), OP.mult)
+        trans(quad("tl", 0, 32, 3), quad(lst, 0, 32, 3))
+        scan(v("ds"), v("md"), v("w7%d" % r), 0.0, OP.mult, OP.add)
+        copy(quad("qe", 0, 16, 3), quad("tl", 0, 16, 3))
+        tt(v("qa", 0, 32, 1, 64, 128), compact(512, 64, 128), compact(512, 0, 64), OP.add)
+        tt(quad("qb", 0, 32, 3), quad("qa", 0, 32, 3), quad("qa", 0, 32, 2), OP.add)
+        trans(quad("qt", 0, 32, 3), quad("qb", 0, 32, 3))
+        tt(quad("qe", 16, 32, 3), quad("qt", 0, 16, 3), quad("qt", 16, 32, 3), OP.add)
+        trans(quad("tr7", 0, 32, 3), quad("qe", 0, 32, 3))
+        ts(quad("off", 0, 32, 3), quad("tr7", 0, 32, 3), dscp(96, 128), OP.mult)
+        for b in range(1, 4):
             sgather(v("pa%d" % b), v("fh%d" % b), v("off", 0, 16))
+        vgather(v("pa0"), v("fh0"), v("off", 0, 16))
+        for b in (1, 0, 2, 3):
             ttg(v("zt", b, 1024, 4), v("fh%d" % b), v("off", 16, 32), v("pa%d" % b))
         quant(v("zq"), v("zqs"), v("zt"))
         rid, pid, _s = topo.addr(nxt)
@@ -524,7 +534,7 @@ def rank_program(g, core, T, topo):
         if r < R - 1:
             for B in range(8):
                 h = 16 * group_of(B)
-                dma("y", "db%d" % r, 8, v("tbf", 0, 4, 1, h, h + 16), v("tr7", 4 * B, 4 * B + 4, 1, 0, 16))
+                dma("y", "db%d" % r, 8, v("tbf", 0, 4, 1, h, h + 16), v("tr7", 4 * B, 4 * B + 4, 1, 112, 128))
         act(v("f0"), v("b0"))
         act(v("f1"), v("b1"))
         scatter(v("posw"), v("off"), v("iotm"))

@@ -5,6 +5,7 @@ EPS = 2.0 ** -120
 SEP = 64.0
 DIG = 2.0 ** 14
 R = 3
+WID = {0: 2, 1: 4, 2: 8, 3: 16, 4: 32}
 
 SCRATCH = {}
 PLACE = {}
@@ -25,8 +26,8 @@ def _part(name, cols, arena="ar"):
 for _n, _c in (("n16", 512), ("i17", 68), ("iot", 512), ("iotm", 512), ("io4", 4), ("bff", 16), ("sgk", 32), ("rtab", 4),
                ("mh", 64), ("md", 512), ("mda", 512), ("t2", 64), ("msk3", 68), ("msk4", 132), ("msk5", 260),
                ("c0", 68), ("c1", 68), ("c2", 68), ("c3", 68), ("c4", 132), ("c5", 260), ("c6", 516), ("c7", 1028),
-               ("kk", 64), ("gm", 64), ("kd", 64), ("sm", 260), ("no", 256), ("np", 256), ("gg", 512), ("hh", 64), ("g5", 64), ("g6", 128), ("o5", 64), ("o6", 64),
-               ("jk", 1028), ("sum4", 4), ("sh", 32), ("shs", 128), ("aa", 32), ("a5", 8), ("ap6", 32), ("tr", 32), ("sw", 32), ("tr2", 32),
+               ("kk", 64), ("gm", 64), ("kd", 64), ("sm", 260), ("no", 256), ("np", 256), ("gg", 512), ("hh", 64), ("g5", 64), ("o5", 64), ("o6", 64),
+               ("jk", 1028), ("sum4", 4), ("sh", 32), ("shs", 128), ("a5", 8), ("ap6", 32), ("tr", 32), ("sw", 64), ("tr2", 64),
                ("qa", 32), ("qb", 32), ("qt", 32), ("qe", 32), ("tl", 32), ("tr7", 32),
                ("id6", 64), ("id7", 64), ("posw", 512), ("pds", 512), ("lr", 20), ("tbf", 4), ("idw", 64), ("ds", 512)):
     _part(_n, _c)
@@ -94,7 +95,7 @@ def rank_program(g, core, T, topo):
         name, at, cols = PLACE[name]
         c0, c1 = c0 + at, (cols if c1 is None else c1) + at
         ap = T[name][p0:p1, c0:c1] if st == 1 else T[name][p0:p1, c0:c1:st]
-        return (name, p0, p1, c0, c1, ap)
+        return (name, p0, p1, c0, c1, ap, st)
 
     def quad(name, c0, c1, a):
         return v(name, c0, c1, 1, 32 * a, 32 * a + 32)
@@ -102,23 +103,23 @@ def rank_program(g, core, T, topo):
     def deps(q, ins, outs):
         toks = {}
         for w, views in ((0, ins), (1, outs)):
-            for n, p0, p1, c0, c1, ap in views:
+            for n, p0, p1, c0, c1, ap, st in views:
                 ps = n in SCRATCH and SCRATCH[n][0] == "psum"
-                for (tok, eng, hw, a, b, c, d) in hist.get(n, []):
-                    if ps and eng != q or (w or hw) and a < p1 and p0 < b and c < c1 and c0 < d:
+                for (tok, eng, hw, a, b, c, d, s) in hist.get(n, []):
+                    if ps and eng != q or (w or hw) and a < p1 and p0 < b and c < c1 and c0 < d and not (s == st > 1 and (c - c0) % st):
                         toks[tok[0]] = max(toks.get(tok[0], 0), tok[1])
         for s in sorted(toks):
             need(q, (s, toks[s]))
 
     def note(q, tok, ins, outs):
         for w, views in ((0, ins), (1, outs)):
-            for n, p0, p1, c0, c1, ap in views:
+            for n, p0, p1, c0, c1, ap, st in views:
                 h = hist.setdefault(n, [])
                 if w:
-                    h[:] = [e for e in h if not (p0 <= e[3] and e[4] <= p1 and c0 <= e[5] and e[6] <= c1)]
+                    h[:] = [e for e in h if not (st in (1, e[7]) and p0 <= e[3] and e[4] <= p1 and c0 <= e[5] and e[6] <= c1 and (e[5] - c0) % st == 0)]
                 else:
-                    h[:] = [e for e in h if not (e[1] == q and not e[2] and e[0][0] == tok[0] and e[3:] == (p0, p1, c0, c1))]
-                h.append((tok, q, w, p0, p1, c0, c1))
+                    h[:] = [e for e in h if not (e[1] == q and not e[2] and e[0][0] == tok[0] and e[3:] == (p0, p1, c0, c1, st))]
+                h.append((tok, q, w, p0, p1, c0, c1, st))
 
     def op(q, fn, outs, ins):
         deps(q, ins, outs)
@@ -128,14 +129,15 @@ def rank_program(g, core, T, topo):
         note(q, (semof[q], count[q]), ins, outs)
 
     def dma(q, sem, group, out, in_):
+        out, in_ = [a if len(a) > 6 else a + (1,) for a in (out, in_)]
         deps(q, [in_], [out])
         queues[q].dma_start(out[5], in_[5]).then_inc(T.sem[sem], 16)
         total[sem] = 16 * group
         note(q, (sem, 16 * group), [in_], [out])
 
     def cd(name):
-        n, p0, p1, a, b, ap = v(name)
-        return (n, p0, p1, a, b, ap.bitcast(dt.uint8))
+        n, p0, p1, a, b, ap, st = v(name)
+        return (n, p0, p1, a, b, ap.bitcast(dt.uint8), 1)
 
     def ts(out, in0, s1, op0, s2=None, op1=None):
         ins = [in0] + [s for s in (s1, s2) if isinstance(s, tuple)]
@@ -190,6 +192,9 @@ def rank_program(g, core, T, topo):
         else:
             op("g", lambda e: e.iota(out[5], pat, base, cm, allow_small_or_imprecise_dtypes=True), [out], [])
 
+    def select(out, in_, pat, fill_, base, cm):
+        op("g", lambda e: e.affine_select(out[5], in_[5], pat, OP.is_equal, fill_, base, cm), [out], [in_])
+
     def group_of(B):
         return 2 * (B % 4) + B // 4
 
@@ -211,12 +216,12 @@ def rank_program(g, core, T, topo):
     iota(v("iot"), [[1, 512]])
     fill(v("ones"), 1.0)
     for b in range(4):
-        o, i = v("ee", 512 * b, 512 * b + 512), v("ones")
-        op("g", lambda e: e.affine_select(o[5], i[5], [[-1, 512]], OP.is_equal, 0.0, b, 4), [o], [i])
+        select(v("ee", 512 * b, 512 * b + 512), v("ones"), [[-1, 512]], 0.0, b, 4)
     iota(v("n16", 64, 512), [[0, 28], [1, 16]])
     iota(v("ap6"), [[0, 32]])
     for r in range(R):
-        for n, c in (("w5s%d", 128), ("w5%d", 128), ("w6%d", 256), ("w7%d", 512), ("list%d", 32)):
+        select(v("w5s%d" % r), v("iot", 0, 128), [[0, 128]], BIG, -1, 0)
+        for n, c in (("w5%d", 128), ("w6%d", 256), ("w7%d", 512), ("list%d", 32)):
             iota(v(n % r), [[0, c]])
     iota(v("iotm"), [[0, 2], [1, 256]])
 
@@ -225,83 +230,107 @@ def rank_program(g, core, T, topo):
         op("v", lambda e: e.tensor_copy(o[5].bitcast(dt.uint32), w[5].bitcast(dt.uint32).indirect(f[5])), [o], [w, f])
         sgather(v("ucs", 128 * a, 128 * b), v("uqs"), f)
 
-    WID = {0: 2, 1: 4, 2: 8, 3: 16, 4: 32}
-    for k in range(5):
-        fill(v("rst%d" % k), -BIG)
-    for n in ("msk3", "msk4", "msk5"):
-        fill(v(n), 1.0)
-    for j, m in enumerate((15, 2, 4, 8, 32, 64, 16, 14, 12)):
-        ts(v("bi", j, j + 1), v("pi"), m, OP.bitwise_and)
-    for k, w in WID.items():
-        fill(v("rst%d" % k, 0, 64, w), BIG)
-    fill(v("msk3", 0, 68, 17), 0.0)
-    fill(v("msk4", 0, 132, 33), 0.0)
-    fill(v("msk5", 0, 260, 65), 0.0)
-    copy(v("bff", 0, 9), v("bi", 0, 9))
-    copy(v("uo"), v("uoi"))
-    q = v("bff", 0, 1)
     col = [0]
 
     def newcol():
         col[0] += 1
         return v("sgk", col[0] - 1, col[0])
 
-    dsc, q1, e6, e7 = newcol(), newcol(), newcol(), newcol()
-
     def dscp(a, b):
         return v("sgk", 0, 1, 1, a, b)
 
+    q = v("bff", 0, 1)
+    dsc, q1, e6, e7 = newcol(), newcol(), newcol(), newcol()
     bit, th, rs0, rs, rw = {}, {}, {}, {}, {}
-    ts(dsc, q, 15.0, OP.is_equal, 1.0 - 1.0 / DIG, OP.mult)
-    ts(q1, q, 1.0, OP.add)
-    ts(v("rtab"), v("io4"), q, OP.add)
-    for k, c, m in ((0, 1, 2), (1, 2, 4), (2, 3, 8), (5, 4, 32), (6, 5, 64), (7, 6, 16)):
+    for k, c in ((0, 1), (1, 2), (2, 3), (5, 4), (6, 5), (7, 6)):
         bit[k], th[k] = v("bff", c, c + 1), newcol()
-        ts(th[k], bit[k], -EPS / m, OP.mult)
     lo = {0: v("bff", 7, 8), 1: v("bff", 8, 9), 2: bit[2]}
     for k in range(3):
         rs0[k], rs[k], rw[k] = newcol(), newcol(), newcol()
-        ts(rs0[k], bit[k], -2.0, OP.mult, lo[k], OP.add)
-        ts(v("t1%d" % k), v("n16", 0, 64), lo[k], OP.is_ge)
+    spare = []
+
+    def later(f, *a):
+        spare.append((f, a))
+
+    def fit(n):
+        for f, a in spare[:n]:
+            f(*a)
+        del spare[:n]
+
+    def masks(k):
+        m, t, s, u = "mq%d" % k, "t1%d" % k, "ms%d" % k, "t3%d" % k
+        later(ts, rs0[k], bit[k], -2.0, OP.mult, lo[k], OP.add)
+        later(ts, v(t), v("n16", 0, 64), lo[k], OP.is_ge)
+        later(ts, v("c%d" % k, 16, 68, 17), v("rtab"), bit[k], OP.subtract, SEP, OP.mult)
+        later(fill, v("rst%d" % k), -BIG)
+        later(ts, rs[k], rs0[k], float(WID[k]), OP.add)
+        later(ts, rw[k], rs0[k], 2.0 * WID[k], OP.add)
+        later(tt, v(m), v(t), v("t2"), OP.mult)
+        later(fill, v("rst%d" % k, 0, 64, WID[k]), BIG)
+        later(ts, v(s), v("i17"), rs[k], OP.not_equal)
+        later(ts, v(u), v("i17"), rw[k], OP.is_equal, SEP - 1.0, OP.mult)
+        later(ts, v(m), v(m), BIG, OP.add)
+        later(tt, v(s), v(s), v(u), OP.add)
+        later(fill, v(s, 0, 68, 17), 0.0)
+
+    def masks3():
+        later(fill, v("msk3"), 1.0)
+        later(ts, v("mh"), v("n16", 0, 64), q, OP.is_equal, -2 * BIG, OP.mult)
+        later(copy, v("c3", 16, 68, 34), v("rtab", 0, 4, 2))
+        later(ts, v("c3", 33, 68, 34), v("rtab", 1, 4, 2), -16.0, OP.add)
+        later(fill, v("msk3", 0, 68, 17), 0.0)
+        later(ts, v("mh"), v("mh"), BIG, OP.add)
+
+    def masks4():
+        later(fill, v("rst4"), -BIG)
+        later(fill, v("msk4"), 1.0)
+        later(copy, v("c4", 32, 66, 33), v("rtab", 0, 2))
+        later(ts, v("c4", 98, 132, 33), v("rtab", 2, 4), -32.0, OP.add)
+        later(fill, v("rst4", 0, 64, 32), BIG)
+        later(fill, v("msk4", 0, 132, 33), 0.0)
+
+    def places(a, b):
+        for c in range(a, b, 64):
+            later(ts, v("mda", c, c + 64), v("n16", c, c + 64), q1, OP.is_equal, DIG - 1.0, OP.mult)
+            later(ts, v("md", c, c + 64), v("n16", c, c + 64), q, OP.is_gt)
+        for c in range(a, b, 64):
+            later(tt, v("md", c, c + 64), v("md", c, c + 64), v("mda", c, c + 64), OP.add)
+
+    def masks5():
+        later(fill, v("msk5"), 1.0)
+        later(copy, v("c5", 64, 260, 65), v("rtab"))
+        later(ts, e6, bit[5], 2.0, OP.mult)
+        later(fill, v("msk5", 0, 260, 65), 0.0)
+        later(ts, e7, bit[6], 2.0, OP.mult, e6, OP.add)
+        later(ts, v("c6", 128, 516, 129), v("rtab"), e6, OP.add)
+        later(ts, v("c7", 256, 1028, 257), v("rtab"), e7, OP.add)
+        places(64, 128)
+
+    def units(k):
+        o, i = 128 * k, 512 * k
+        later(quant, v("eq", o, o + 128), v("eqs", o, o + 128), v("ee", i, i + 512))
+
+    for j, m in enumerate((15, 2, 4, 8, 32, 64, 16, 14, 12)):
+        ts(v("bi", j, j + 1), v("pi"), m, OP.bitwise_and)
+    fill(v("rst3"), -BIG)
+    copy(v("bff", 0, 9), v("bi", 0, 9))
+    fill(v("rst3", 0, 64, 16), BIG)
+    copy(v("uo"), v("uoi"))
+    ts(dsc, q, 15.0, OP.is_equal, 1.0 - 1.0 / DIG, OP.mult)
+    ts(q1, q, 1.0, OP.add)
+    ts(v("rtab"), v("io4"), q, OP.add)
     ts(v("t2"), v("n16", 0, 64), q, OP.is_le, -2 * BIG, OP.mult)
-    ts(v("mh"), v("n16", 0, 64), q, OP.is_equal, -2 * BIG, OP.mult)
     ts(v("md", 0, 64), v("n16", 0, 64), q, OP.is_gt)
-    ts(e6, bit[5], 2.0, OP.mult)
+    for k, m in ((0, 2), (1, 4), (2, 8), (5, 32), (6, 64), (7, 16)):
+        ts(th[k], bit[k], -EPS / m, OP.mult)
     ts(dsc, dsc, 1.0 / DIG, OP.add)
-    for k in range(3):
-        ts(rs[k], rs0[k], float(WID[k]), OP.add)
-        ts(rw[k], rs0[k], 2.0 * WID[k], OP.add)
-        tt(v("mq%d" % k), v("t1%d" % k), v("t2"), OP.mult)
-        ts(v("c%d" % k, 16, 68, 17), v("rtab"), bit[k], OP.subtract, SEP, OP.mult)
     ts(v("mda", 0, 64), v("n16", 0, 64), q1, OP.is_equal, DIG - 1.0, OP.mult)
-    ts(v("mh"), v("mh"), BIG, OP.add)
-    for k in range(3):
-        ts(v("mq%d" % k), v("mq%d" % k), BIG, OP.add)
-        ts(v("ms%d" % k), v("i17"), rs[k], OP.not_equal)
-        ts(v("t3%d" % k), v("i17"), rw[k], OP.is_equal, SEP - 1.0, OP.mult)
+    masks(0)
+    fit(99)
     tt(v("md", 0, 64), v("md", 0, 64), v("mda", 0, 64), OP.add)
-    for k in range(3):
-        tt(v("ms%d" % k), v("ms%d" % k), v("t3%d" % k), OP.add)
     quant(v("uq"), v("uqs"), v("ut"))
     upick(0, 1)
-
-    def rest():
-        for k in range(3):
-            fill(v("ms%d" % k, 0, 68, 17), 0.0)
-        copy(v("c3", 16, 68, 34), v("rtab", 0, 4, 2))
-        ts(v("c3", 33, 68, 34), v("rtab", 1, 4, 2), -16.0, OP.add)
-        copy(v("c4", 32, 66, 33), v("rtab", 0, 2))
-        ts(v("c4", 98, 132, 33), v("rtab", 2, 4), -32.0, OP.add)
-        ts(e7, bit[6], 2.0, OP.mult, e6, OP.add)
-        copy(v("c5", 64, 260, 65), v("rtab"))
-        ts(v("c6", 128, 516, 129), v("rtab"), e6, OP.add)
-        ts(v("c7", 256, 1028, 257), v("rtab"), e7, OP.add)
-
-    def wide():
-        ts(v("mda", 64, 512), v("n16", 64, 512), q1, OP.is_equal, DIG - 1.0, OP.mult)
-        ts(v("md", 64, 512), v("n16", 64, 512), q, OP.is_gt)
-        quant(v("vq"), v("vqs"), v("vt"))
-        tt(v("md", 64, 512), v("md", 64, 512), v("mda", 64, 512), OP.add)
+    masks(1)
 
     def compact(c1, p0=0, p1=128):
         return v("ds", 15, c1, 16, p0, p1)
@@ -320,36 +349,27 @@ def rank_program(g, core, T, topo):
         def score(k, bank, c0=0, c1=512):
             mm(v(bank, 0, c1 - c0), v("uc", 128 * k, 128 * k + 128), v("ucs", 128 * k, 128 * k + 128), v("xq", c0, c1), v("xqs", c0, c1))
 
+        def scored(k, bank):
+            act(v("sw%d" % k), v(bank), -1.0)
+
         def unpack(b):
             mm(v("b%d" % b), v("eq", 128 * b, 128 * b + 128), v("eqs", 128 * b, 128 * b + 128), v("xq"), v("xqs"))
+
+        def half(b):
+            act(v("fh%d" % b), v("b%d" % b), 0.5)
 
         score(0, "b4", 0, 256)
         score(0, "b5", 256, 512)
         if r == 0:
-            upick(1, 2)
+            upick(1, 4)
         ts(v("sw0", 0, 256), v("b4", 0, 256), -1.0, OP.mult)
         act(v("sw0", 256, 512), v("b5", 0, 256), -1.0)
-        if r == 0:
-            rest()
+        fit(3)
         vgather(v("g0"), v("sw0"), v("tb"))
+        fit(3)
         score(1, "b6")
-        act(v("sw1"), v("b6"), -1.0)
+        scored(1, "b6")
         sgather(v("o1"), v("sw1"), v("tb"))
-        if r == 0:
-            upick(2, 8)
-        score(2, "b7")
-        act(v("sw2"), v("b7"), -1.0)
-        score(3, "b4")
-        if r == 0:
-            for b in range(4):
-                quant(v("eq", 128 * b, 128 * b + 128), v("eqs", 128 * b, 128 * b + 128), v("ee", 512 * b, 512 * b + 512))
-        unpack(0)
-        score(4, "b5")
-        unpack(1)
-        score(5, "b6")
-        unpack(2)
-        score(6, "b7")
-        unpack(3)
 
         def tail(k, part):
             dst = "idw" if k == 4 else "id%dr" % (k + 1)
@@ -365,7 +385,7 @@ def rank_program(g, core, T, topo):
                 dma("y", "dga%d%d" % (r, k), 1, ("dg%d" % r, 0, 128, k, k + 1, dg[k]), v("lr", 4 * k, 4 * k + 4))
 
         for k in range(5):
-            w = 2 << k
+            w = WID[k]
             G = v("g%d" % k)
             C = "c%d" % k
             if k < 3:
@@ -380,6 +400,7 @@ def rank_program(g, core, T, topo):
                 scan(v("kd"), v("mh"), v("kk"), BIG, OP.min, OP.max)
             if k:
                 tail(k - 1, 1)
+            fit(3)
             s = 17 if k < 3 else w + 1
             for c in range(4):
                 x = v("kd", 16 * c + 15, 16 * c + 16)
@@ -389,29 +410,70 @@ def rank_program(g, core, T, topo):
                     left = c % 2 == 0 if k == 3 else c < 2
                     a = 16 * (c ^ 1) if k == 3 else 32 * left
                     ts(v(C, s * c, s * c + w), v("kk", a, a + w), x, OP.is_gt if left else OP.is_ge)
-            scan(v("sm", 0, 4 * s), v(("ms%d" if k < 3 else "msk%d") % k), v(C), 0.0, OP.mult, OP.add)
             if k:
                 tail(k - 1, 2)
+            scan(v("sm", 0, 4 * s), v(("ms%d" if k < 3 else "msk%d") % k), v(C), 0.0, OP.mult, OP.add)
+            fit(4)
             if k < 3:
                 ts(v("rk"), v("sm", 16, 68, 17), 1.0 / SEP, OP.mult)
             else:
                 copy(v("rk"), v("sm", w, 4 * s, s))
+            fit(4)
             scatter(v("g%d" % (k + 1)), v("rk"), v("o%d" % (k + 1)))
-            if k == 0:
-                act(v("sw3"), v("b4"), -1.0)
+            fit(99)
+            if r == 0:
+                if k == 0:
+                    score(2, "b7")
+                    score(3, "b4")
+                    scored(2, "b7")
+                    scored(3, "b4")
+                    masks(2)
+                    later(upick, 4, 5)
+                    masks3()
+                elif k == 1:
+                    score(4, "b5")
+                    scored(4, "b5")
+                    later(upick, 5, 6)
+                    masks4()
+                    units(0)
+                    units(1)
+                elif k == 2:
+                    score(5, "b6")
+                    scored(5, "b6")
+                    unpack(0)
+                    later(upick, 6, 8)
+                    units(2)
+                    units(3)
+                elif k == 3:
+                    score(6, "b7")
+                    scored(6, "b7")
+                    score(7, "b4")
+                    for b in range(1, 4):
+                        unpack(b)
+                    masks5()
+                else:
+                    scored(7, "b4")
+                    half(0)
+            elif k == 0:
+                score(2, "b7")
+                scored(2, "b7")
+                score(3, "b4")
+                for b in range(4):
+                    unpack(b)
+                    if b < 3:
+                        score(b + 4, "b%d" % (b + 5))
+                scored(3, "b4")
                 score(7, "b4")
-                act(v("fh0"), v("b0"), 0.5)
+                half(0)
             elif k < 3:
-                act(v("sw%d" % (k + 3)), v("b%d" % (k + 4)), -1.0)
-                act(v("fh%d" % k), v("b%d" % k), 0.5)
+                scored(k + 3, "b%d" % (k + 4))
+                half(k)
             elif k == 3:
-                act(v("sw6"), v("b7"), -1.0)
-                act(v("sw7"), v("b4"), -1.0)
-            if r == 0 and k == 1:
-                wide()
+                scored(6, "b7")
+                scored(7, "b4")
 
-        def runmin(out, in_):
-            scan(out, in_, in_, BIG, OP.min, OP.min)
+        def runmin(out, a, b=None):
+            scan(out, a, b or a, BIG, OP.min, OP.min)
 
         def hold(w):
             if w == 64:
@@ -455,15 +517,20 @@ def rank_program(g, core, T, topo):
         for c in range(4):
             versus(5, 64, c)
         tail(4, 2)
+        fit(99)
+        if r == 0:
+            places(128, 512)
+            later(quant, v("vq"), v("vqs"), v("vt"))
         scan(v("sm"), v("msk5"), v("c5"), 0.0, OP.mult, OP.add)
         copy(v("rk"), v("sm", 64, 260, 65))
+        fit(3)
         scatter(v("w5s%d" % r), v("rk"), v("o6"))
         swap1("shs", "w5s%d" % r, 128)
         scatter(v("w5%d" % r), v("rk"), v("idw"))
-        tt(v("g6"), v("w5s%d" % r), v("shs"), OP.add)
+        runmin(v("no", 0, 128), v("w5s%d" % r), v("shs"))
         scan(v("ds", 0, 128), v("md", 0, 128), v("w5%d" % r), 0.0, OP.mult, OP.add)
-        runmin(v("no", 0, 128), v("g6"))
         swap2("np", "no", 128)
+        fit(3)
         hold(128)
         swap1("sh", "ds", 8, dsq)
         versus(6, 128, 0)
@@ -472,6 +539,7 @@ def rank_program(g, core, T, topo):
         versus(6, 128, 2)
         versus(6, 128, 3)
         owns("own6", "a5", 2)
+        fit(8)
         sgather(v("id6"), v("iot"), v("own6"))
         ts(v("rk"), v("sum4"), 1.0, OP.mult)
         scatter(v("w6%d" % r), v("rk"), v("id6"))
@@ -481,29 +549,33 @@ def rank_program(g, core, T, topo):
         for B in range(8):
             h = 16 * group_of(B)
             dma("y", "dl%d" % r, 8, v(lst, 4 * B, 4 * B + 4, 1, 0, 80), ("dg%d" % r, h, h + 16, 0, 5, dg[0:5, h:h + 16, :]))
+        fit(99)
         scan(v("ds", 0, 256), v("md", 0, 256), v("w6%d" % r), 0.0, OP.mult, OP.add)
         swap1("sh", "ds", 16, dsq)
-        tt(v("aa", 0, 16), compact(256), v("sh", 0, 16), OP.add)
-        swap2("sh", "aa", 16)
-        tt(v("ap6", 0, 16), v("aa", 0, 16), v("sh", 0, 16), OP.add)
+        tt(v("ap6", 0, 16), compact(256), v("sh", 0, 16), OP.add)
         trans(v("tr"), v("ap6"))
-        ts(v("tab7", 0, 16), v("ap6", 0, 16), dsc, OP.mult)
-        copy(v("sw", 0, 16), v("tr", 16, 32))
-        copy(v("sw", 16, 32), v("tr", 0, 16))
+        swap2("sh", "tr", 32)
+        tt(v("sw", 32, 48), v("tr", 16, 32), v("sh", 16, 32), OP.add)
+        tt(v("sw", 48, 64), v("tr", 0, 16), v("sh", 0, 16), OP.add)
+        tt(v("sw", 0, 32), v("tr"), v("sh"), OP.add)
         trans(v("tr2"), v("sw"))
-        owns("own7", "ap6", 4)
-        ts(v("tab7", 16, 32), v("tr2", 0, 16), dsc, OP.mult)
+        ts(v("tab7", 16, 32), v("tr2", 32, 48), dsc, OP.mult)
+        ts(v("tab7", 0, 16), v("tr2", 0, 16), dsc, OP.mult)
         for j in range(2):
-            dma("y", "dn%d" % r, 2, v(lst, 16 * j, 16 * j + 16, 1, 96, 112), v("ap6", 0, 16, 1, 16 * j, 16 * j + 16))
+            dma("y", "dn%d" % r, 2, v(lst, 16 * j, 16 * j + 16, 1, 96, 112), v("tr2", 0, 16, 1, 16 * j, 16 * j + 16))
         sgather(v("gg", 256, 512), v("sw7"), v("tab7", 16, 32))
         vgather(v("gg", 0, 256), v("sw7"), v("tab7", 0, 16))
+        owns("own7", "tr2", 4)
         sgather(v("id7"), v("iot"), v("own7"))
         runmin(v("no"), v("gg", 0, 256))
         runmin(v("np"), v("gg", 256, 512))
         hold(256)
         for c in range(4):
             versus(7, 256, c)
-        act(v("fh3"), v("b3"), 0.5)
+        if r == 0:
+            half(1)
+            half(2)
+        half(3)
         ts(v("rk"), v("sum4"), 1.0, OP.mult)
         scatter(v("w7%d" % r), v("rk"), v("id7"))
         ts(v("off", 0, 32, 1, 0, 96), v(lst, 0, 32, 1, 0, 96), dscp(0, 96), OP.mult)
@@ -543,25 +615,28 @@ def rank_program(g, core, T, topo):
         if r == R - 1:
             sgather(v("row"), v("iot"), v("off"))
             dma("y", "dod", 1, ("od", 0, 8, 0, 512, T.od[:, :]), ("row", 0, 128, 0, 512, T.row[0:128:16, :]))
-        for b in range(4):
+        for b in (0, 2, 1, 3):
             mm(v("b%d" % (4 + b), 0, 256), v("wq", 128 * b, 128 * b + 128), v("wqs", 128 * b, 128 * b + 128), v("zl%d" % r), v("zl%ds" % r))
-        ts(v("pp0"), v("b4", 0, 256), 0.03125, OP.mult)
-        act(v("pp1"), v("b5", 0, 256), 0.03125)
-        act(v("pp2"), v("b6", 0, 256), 0.03125)
-        sgather(v("gp2"), v("pp2"), v("pos"))
-        act(v("pp3"), v("b7", 0, 256), 0.03125)
-        sgather(v("gp3"), v("pp3"), v("pos"))
-        for b in range(2):
+        for b in (2, 3):
+            act(v("pp%d" % b), v("b%d" % (4 + b), 0, 256), 0.03125)
+        for b in (0, 1):
+            ts(v("pp%d" % b), v("b%d" % (4 + b), 0, 256), 0.03125, OP.mult)
+        for b in (2, 3):
+            sgather(v("gp%d" % b), v("pp%d" % b), v("pos"))
+        for b in (0, 1):
             ttg(v("xt", b, 2048, 4), v("pp%d" % b), v("pos"), v("f%d" % b))
-        for b in range(2, 4):
-            tt(v("xt", b, 2048, 4), v("gp%d" % b), v("b%d" % b), OP.add)
+        for b in (2, 3):
+            for c in (0, 256):
+                tt(v("xt", 4 * c + b, 4 * c + 1024, 4), v("gp%d" % b, c, c + 256), v("b%d" % b, c, c + 256), OP.add)
 
-    quant(v("xq"), v("xqs"), v("xt"))
-    mm(v("b4"), v("vq"), v("vqs"), v("xq"), v("xqs"))
+    for c in (0, 256):
+        quant(v("xq", c, c + 256), v("xqs", c, c + 256), v("xt", 4 * c, 4 * c + 1024))
+        mm(v("b4" if c == 0 else "b5", 0, 256), v("vq"), v("vqs"), v("xq", c, c + 256), v("xqs", c, c + 256))
     dma("y", "doc", 1, ("oc", 0, 128, 0, 2048, T.oc[:, :]), cd("xq"))
     for k in range(4):
         dma("y", "dos", 4, ("osc", 4 * k, 4 * k + 4, 0, 512, T.osc[4 * k:4 * k + 4, :]), v("xqs", 0, 512, 1, 32 * k, 32 * k + 4))
-    act(v("yy"), v("b4"))
+    copy(v("yy", 0, 256), v("b4", 0, 256))
+    act(v("yy", 256, 512), v("b5", 0, 256))
     dma("y", "dy", 1, ("y", 0, 128, 0, 512, T.y[:, :]), v("yy"))
     for k in semof:
         need("g", (semof[k], count[k]))

from concourse.mybir import dt, AluOpType as OP, ActivationFunctionType as AF

BIG = 2.0 ** 75
EPS = 2.0 ** -120
SEP = 64.0
DIG = 2.0 ** 14
R = 3
WID = {0: 2, 1: 4, 2: 8, 3: 16, 4: 32}

SCRATCH = {}
PLACE = {}
_used = {"ar": 0, "ar16": 0}
SEMAPHORES = ["sv", "ss", "sp", "sg", "dx0", "dx1", "du", "dv", "dp", "dw", "doc", "dos", "dod", "dy"]


def _buf(name, cols, dtype="float32", where="sbuf"):
    SCRATCH[name] = (where, [128, cols], dtype)
    PLACE[name] = (name, 0, cols)


def _part(name, cols, arena="ar"):
    PLACE[name] = (arena, _used[arena], cols)
    _used[arena] += -(-cols // 16) * 16


for _n, _c in (("n16", 512), ("i17", 68), ("iot", 512), ("iotm", 512), ("io4", 4), ("bff", 16), ("sgk", 32), ("rtab", 4),
               ("mh", 64), ("md", 512), ("mda", 512), ("t2", 64), ("msk3", 68), ("msk4", 132), ("msk5", 260),
               ("c0", 68), ("c1", 68), ("c2", 68), ("c3", 68), ("c4", 132), ("c5", 260), ("c6", 516), ("c7", 1028),
               ("kk", 64), ("gm", 64), ("kd", 64), ("sm", 260), ("no", 256), ("np", 256), ("gg", 512), ("hh", 64), ("g5", 64), ("o5", 64), ("o6", 64),
               ("jk", 1028), ("sum4", 4), ("sh", 32), ("shs", 128), ("a5", 8), ("ap6", 32), ("tr", 32), ("sw", 64), ("tr2", 64),
               ("qa", 32), ("qb", 32), ("qt", 32), ("qe", 32), ("tl", 32), ("tr7", 32),
               ("id6", 64), ("id7", 64), ("posw", 512), ("pds", 512), ("lr", 20), ("tbf", 4), ("idw", 64), ("ds", 512)):
    _part(_n, _c)
for _g in range(5):
    for _s in ("g%d", "o%d", "id%dr", "rst%d"):
        if _s != "o%d" or _g:
            _part(_s % _g, 64)
for _g in range(3):
    for _s, _c in (("mq%d", 64), ("ms%d", 68), ("t1%d", 64), ("t3%d", 68)):
        _part(_s % _g, _c)
for _r in range(R):
    _part("list%d" % _r, 32)
    for _s, _c in (("w5s%d", 128), ("w5%d", 128), ("w6%d", 256), ("w7%d", 512)):
        _part(_s % _r, _c)
    SCRATCH["dg%d" % _r] = ("dram", [5, 128, 4], "float32")
for _n, _c in (("uo", 64), ("rk", 4), ("tb", 4), ("tab5", 4), ("tab7", 32), ("own6", 4), ("own7", 4), ("off", 32), ("pos", 32),
               ("tbl0", 4), ("tbl1", 4), ("tbl2", 4), ("tbl3", 4)):
    _part(_n, _c, "ar16")
_buf("ar", _used["ar"])
_buf("ar16", _used["ar16"], "uint16")
_buf("row", 512)
_buf("yy", 512)
for _g in range(8):
    _buf("sw%d" % _g, 512)
for _b in range(4):
    _buf("fh%d" % _b, 512)
    _buf("pa%d" % _b, 256)
    _buf("pp%d" % _b, 256)
for _b in range(2):
    _buf("f%d" % _b, 512)
    _buf("gp%d" % (_b + 2), 512)
for _n, _c in (("pi", 1), ("bi", 16), ("uoi", 64), ("tbi", 4)):
    _buf(_n, _c, "int32")
for _n, _c in (("xt", 2048), ("ut", 512), ("vt", 512), ("zt", 1024), ("ee", 2048), ("ones", 512)):
    _buf(_n, _c, "bfloat16")
for _n, _c in (("xq", 512), ("uq", 128), ("uc", 1024), ("vq", 128), ("wq", 512), ("zq", 256), ("eq", 512)) + tuple(("zl%d" % r, 256) for r in range(R)):
    _buf(_n, _c, "float8_e4m3fn_x4")
    _buf(_n + "s", _c, "uint8")
for _b in range(8):
    _buf("b%d" % _b, 512, "float32", "psum")
for _r in range(R):
    SEMAPHORES += [s % _r for s in ("ac%d", "as%d", "lc%d", "ls%d", "dl%d", "dm%d", "dn%d", "db%d")]
    SEMAPHORES += ["dga%d%d" % (_r, g) for g in range(5)]


def rank_program(g, core, T, topo):
    rank = T.rank_of(core)
    if rank is None:
        return
    nxt = T.cores[(rank + 1) % len(T.cores)]
    queues = {"v": g.vector, "s": g.scalar, "t": g.tensor, "g": g, "y": g.sync}
    semof = {"v": "sv", "s": "ss", "t": "sp", "g": "sg"}
    count = {k: 0 for k in semof}
    known = {k: {} for k in queues}
    hist = {}
    total = {}

    def need(q, tok):
        sem, val = tok
        if known[q].get(sem, 0) < val:
            queues[q].wait_ge(T.sem[sem], val)
            known[q][sem] = val

    def v(name, c0=0, c1=None, st=1, p0=0, p1=128):
        name, at, cols = PLACE[name]
        c0, c1 = c0 + at, (cols if c1 is None else c1) + at
        ap = T[name][p0:p1, c0:c1] if st == 1 else T[name][p0:p1, c0:c1:st]
        return (name, p0, p1, c0, c1, ap, st)

    def quad(name, c0, c1, a):
        return v(name, c0, c1, 1, 32 * a, 32 * a + 32)

    def deps(q, ins, outs):
        toks = {}
        for w, views in ((0, ins), (1, outs)):
            for n, p0, p1, c0, c1, ap, st in views:
                ps = n in SCRATCH and SCRATCH[n][0] == "psum"
                for (tok, eng, hw, a, b, c, d, s) in hist.get(n, []):
                    if ps and eng != q or (w or hw) and a < p1 and p0 < b and c < c1 and c0 < d and not (s == st > 1 and (c - c0) % st):
                        toks[tok[0]] = max(toks.get(tok[0], 0), tok[1])
        for s in sorted(toks):
            need(q, (s, toks[s]))

    def note(q, tok, ins, outs):
        for w, views in ((0, ins), (1, outs)):
            for n, p0, p1, c0, c1, ap, st in views:
                h = hist.setdefault(n, [])
                if w:
                    h[:] = [e for e in h if not (st in (1, e[7]) and p0 <= e[3] and e[4] <= p1 and c0 <= e[5] and e[6] <= c1 and (e[5] - c0) % st == 0)]
                else:
                    h[:] = [e for e in h if not (e[1] == q and not e[2] and e[0][0] == tok[0] and e[3:] == (p0, p1, c0, c1, st))]
                h.append((tok, q, w, p0, p1, c0, c1, st))

    def op(q, fn, outs, ins):
        deps(q, ins, outs)
        i = fn(queues[q])
        count[q] += 1
        i.then_inc(T.sem[semof[q]], 1)
        note(q, (semof[q], count[q]), ins, outs)

    def dma(q, sem, group, out, in_):
        out, in_ = [a if len(a) > 6 else a + (1,) for a in (out, in_)]
        deps(q, [in_], [out])
        queues[q].dma_start(out[5], in_[5]).then_inc(T.sem[sem], 16)
        total[sem] = 16 * group
        note(q, (sem, 16 * group), [in_], [out])

    def cd(name):
        n, p0, p1, a, b, ap, st = v(name)
        return (n, p0, p1, a, b, ap.bitcast(dt.uint8), 1)

    def ts(out, in0, s1, op0, s2=None, op1=None):
        ins = [in0] + [s for s in (s1, s2) if isinstance(s, tuple)]
        a, b = [s[5] if isinstance(s, tuple) else s for s in (s1, s2)]
        if op1 is None:
            op("v", lambda e: e.tensor_scalar(out[5], in0[5], a, None, op0), [out], ins)
        else:
            op("v", lambda e: e.tensor_scalar(out[5], in0[5], a, b, op0, op1), [out], ins)

    def tt(out, a, b, o):
        op("v", lambda e: e.tensor_tensor(out[5], a[5], b[5], o), [out], [a, b])

    def ttg(out, win, off, b):
        op("v", lambda e: e.tensor_tensor(out[5], win[5].indirect(off[5]), b[5], OP.add), [out], [win, off, b])

    def scan(out, d0, d1, init, o0, o1):
        op("v", lambda e: e.tensor_tensor_scan(out[5], d0[5], d1[5], init, o0, o1), [out], [d0, d1])

    def copy(out, in_):
        op("v", lambda e: e.tensor_copy(out[5], in_[5]), [out], [in_])

    def trans(out, in_):
        op("v", lambda e: e.transpose(out[5], in_[5]), [out], [in_])

    def fill(out, c):
        op("v", lambda e: e.memset(out[5], c), [out], [])

    def vgather(out, win, off):
        op("v", lambda e: e.tensor_copy(out[5], win[5].indirect(off[5])), [out], [win, off])

    def scatter(win, off, in_):
        op("v", lambda e: e.tensor_copy(win[5].indirect(off[5]), in_[5]), [win], [off, in_])

    def act(out, in_, scale=1.0):
        op("s", lambda e: e.activation(out[5], in_[5], AF.Copy, scale=scale), [out], [in_])

    def sgather(out, win, off):
        op("s", lambda e: e.activation(out[5], win[5].indirect(off[5]), AF.Copy), [out], [win, off])

    def accum(out, in_, acc):
        op("s", lambda e: e.activation(out[5], in_[5], AF.Copy, accum_out=acc[5]), [out, acc], [in_])

    def quant(c, s, t):
        op("v", lambda e: e.quantize_mx(c[5], s[5], t[5]), [c, s], [t])

    def mm(out, l, ls, r_, rs):
        op("t", lambda e: e.matmul_mx(out[5], l[5], ls[5], r_[5], rs[5], True, True), [out], [l, ls, r_, rs])

    def iota(out, pat, base=0, cm=0):
        if out[0] in ("pi", "uoi"):
            op("g", lambda e: e.iota(out[5], pat, base, cm), [out], [])
        else:
            op("g", lambda e: e.iota(out[5], pat, base, cm, allow_small_or_imprecise_dtypes=True), [out], [])

    def select(out, in_, pat, fill_, base, cm):
        op("g", lambda e: e.affine_select(out[5], in_[5], pat, OP.is_equal, fill_, base, cm), [out], [in_])

    def group_of(B):
        return 2 * (B % 4) + B // 4

    dma("y", "du", 1, v("ut"), ("u", 0, 128, 0, 512, T.u[:, :]))
    dma("s", "dx0", 1, v("xt", 0, 1024), ("x", 0, 128, 0, 1024, T.x[:, 0:1024]))
    dma("y", "dx1", 1, v("xt", 1024, 2048), ("x", 0, 128, 1024, 2048, T.x[:, 1024:2048]))
    for B in range(8):
        h = 16 * group_of(B)
        dma("y", "dp", 8, v("tbi", 0, 4, 1, h, h + 16), ("p", 0, 16, 4 * B, 4 * B + 4, T.p[:, 4 * B:4 * B + 4]))
    dma("y", "dv", 1, v("vt"), ("v", 0, 128, 0, 512, T.v[:, :]))
    dma("y", "dw", 2, cd("wq"), ("wc", 0, 128, 0, 2048, T.wc[:, :]))
    dma("y", "dw", 2, v("wqs"), ("ws", 0, 128, 0, 512, T.ws[:, :]))

    iota(v("pi"), [[0, 1]], 0, 1)
    iota(v("n16", 0, 64), [[0, 4], [1, 16]])
    iota(v("io4"), [[16, 4]])
    iota(v("i17"), [[0, 4], [1, 17]])
    iota(v("uoi"), [[16, 8], [0, 8]])
    iota(v("iot"), [[1, 512]])
    fill(v("ones"), 1.0)
    for b in range(4):
        select(v("ee", 512 * b, 512 * b + 512), v("ones"), [[-1, 512]], 0.0, b, 4)
    iota(v("n16", 64, 512), [[0, 28], [1, 16]])
    iota(v("ap6"), [[0, 32]])
    for r in range(R):
        select(v("w5s%d" % r), v("iot", 0, 128), [[0, 128]], BIG, -1, 0)
        for n, c in (("w5%d", 128), ("w6%d", 256), ("w7%d", 512), ("list%d", 32)):
            iota(v(n % r), [[0, c]])
    iota(v("iotm"), [[0, 2], [1, 256]])

    def upick(a, b):
        o, w, f = v("uc", 128 * a, 128 * b), v("uq"), v("uo", 8 * a, 8 * b)
        op("v", lambda e: e.tensor_copy(o[5].bitcast(dt.uint32), w[5].bitcast(dt.uint32).indirect(f[5])), [o], [w, f])
        sgather(v("ucs", 128 * a, 128 * b), v("uqs"), f)

    col = [0]

    def newcol():
        col[0] += 1
        return v("sgk", col[0] - 1, col[0])

    def dscp(a, b):
        return v("sgk", 0, 1, 1, a, b)

    q = v("bff", 0, 1)
    dsc, q1, e6, e7 = newcol(), newcol(), newcol(), newcol()
    bit, th, rs0, rs, rw = {}, {}, {}, {}, {}
    for k, c in ((0, 1), (1, 2), (2, 3), (5, 4), (6, 5), (7, 6)):
        bit[k], th[k] = v("bff", c, c + 1), newcol()
    lo = {0: v("bff", 7, 8), 1: v("bff", 8, 9), 2: bit[2]}
    for k in range(3):
        rs0[k], rs[k], rw[k] = newcol(), newcol(), newcol()
    spare = []

    def later(f, *a):
        spare.append((f, a))

    def fit(n):
        for f, a in spare[:n]:
            f(*a)
        del spare[:n]

    def masks(k):
        m, t, s, u = "mq%d" % k, "t1%d" % k, "ms%d" % k, "t3%d" % k
        later(ts, rs0[k], bit[k], -2.0, OP.mult, lo[k], OP.add)
        later(ts, v(t), v("n16", 0, 64), lo[k], OP.is_ge)
        later(ts, v("c%d" % k, 16, 68, 17), v("rtab"), bit[k], OP.subtract, SEP, OP.mult)
        later(fill, v("rst%d" % k), -BIG)
        later(ts, rs[k], rs0[k], float(WID[k]), OP.add)
        later(ts, rw[k], rs0[k], 2.0 * WID[k], OP.add)
        later(tt, v(m), v(t), v("t2"), OP.mult)
        later(fill, v("rst%d" % k, 0, 64, WID[k]), BIG)
        later(ts, v(s), v("i17"), rs[k], OP.not_equal)
        later(ts, v(u), v("i17"), rw[k], OP.is_equal, SEP - 1.0, OP.mult)
        later(ts, v(m), v(m), BIG, OP.add)
        later(tt, v(s), v(s), v(u), OP.add)
        later(fill, v(s, 0, 68, 17), 0.0)

    def masks3():
        later(fill, v("msk3"), 1.0)
        later(ts, v("mh"), v("n16", 0, 64), q, OP.is_equal, -2 * BIG, OP.mult)
        later(copy, v("c3", 16, 68, 34), v("rtab", 0, 4, 2))
        later(ts, v("c3", 33, 68, 34), v("rtab", 1, 4, 2), -16.0, OP.add)
        later(fill, v("msk3", 0, 68, 17), 0.0)
        later(ts, v("mh"), v("mh"), BIG, OP.add)

    def masks4():
        later(fill, v("rst4"), -BIG)
        later(fill, v("msk4"), 1.0)
        later(copy, v("c4", 32, 66, 33), v("rtab", 0, 2))
        later(ts, v("c4", 98, 132, 33), v("rtab", 2, 4), -32.0, OP.add)
        later(fill, v("rst4", 0, 64, 32), BIG)
        later(fill, v("msk4", 0, 132, 33), 0.0)

    def places(a, b):
        for c in range(a, b, 64):
            later(ts, v("mda", c, c + 64), v("n16", c, c + 64), q1, OP.is_equal, DIG - 1.0, OP.mult)
            later(ts, v("md", c, c + 64), v("n16", c, c + 64), q, OP.is_gt)
        for c in range(a, b, 64):
            later(tt, v("md", c, c + 64), v("md", c, c + 64), v("mda", c, c + 64), OP.add)

    def masks5():
        later(fill, v("msk5"), 1.0)
        later(copy, v("c5", 64, 260, 65), v("rtab"))
        later(ts, e6, bit[5], 2.0, OP.mult)
        later(fill, v("msk5", 0, 260, 65), 0.0)
        later(ts, e7, bit[6], 2.0, OP.mult, e6, OP.add)
        later(ts, v("c6", 128, 516, 129), v("rtab"), e6, OP.add)
        later(ts, v("c7", 256, 1028, 257), v("rtab"), e7, OP.add)
        places(64, 128)

    def units(k):
        o, i = 128 * k, 512 * k
        later(quant, v("eq", o, o + 128), v("eqs", o, o + 128), v("ee", i, i + 512))

    for j, m in enumerate((15, 2, 4, 8, 32, 64, 16, 14, 12)):
        ts(v("bi", j, j + 1), v("pi"), m, OP.bitwise_and)
    fill(v("rst3"), -BIG)
    copy(v("bff", 0, 9), v("bi", 0, 9))
    fill(v("rst3", 0, 64, 16), BIG)
    copy(v("uo"), v("uoi"))
    ts(dsc, q, 15.0, OP.is_equal, 1.0 - 1.0 / DIG, OP.mult)
    ts(q1, q, 1.0, OP.add)
    ts(v("rtab"), v("io4"), q, OP.add)
    ts(v("t2"), v("n16", 0, 64), q, OP.is_le, -2 * BIG, OP.mult)
    ts(v("md", 0, 64), v("n16", 0, 64), q, OP.is_gt)
    for k, m in ((0, 2), (1, 4), (2, 8), (5, 32), (6, 64), (7, 16)):
        ts(th[k], bit[k], -EPS / m, OP.mult)
    ts(dsc, dsc, 1.0 / DIG, OP.add)
    ts(v("mda", 0, 64), v("n16", 0, 64), q1, OP.is_equal, DIG - 1.0, OP.mult)
    masks(0)
    fit(99)
    tt(v("md", 0, 64), v("md", 0, 64), v("mda", 0, 64), OP.add)
    quant(v("uq"), v("uqs"), v("ut"))
    upick(0, 1)
    masks(1)

    def compact(c1, p0=0, p1=128):
        return v("ds", 15, c1, 16, p0, p1)

    for r in range(R):
        lst = "list%d" % r
        dg = T["dg%d" % r]
        if r == 0:
            copy(v("tb"), v("tbi"))
        else:
            ts(v("tb"), v("tbf"), dsc, OP.mult)
        quant(v("xq", 0, 256), v("xqs", 0, 256), v("xt", 0, 1024))
        quant(v("xq", 256, 512), v("xqs", 256, 512), v("xt", 1024, 2048))
        sgather(v("id0r"), v("iot"), v("tb"))

        def score(k, bank, c0=0, c1=512):
            mm(v(bank, 0, c1 - c0), v("uc", 128 * k, 128 * k + 128), v("ucs", 128 * k, 128 * k + 128), v("xq", c0, c1), v("xqs", c0, c1))

        def scored(k, bank):
            act(v("sw%d" % k), v(bank), -1.0)

        def unpack(b):
            mm(v("b%d" % b), v("eq", 128 * b, 128 * b + 128), v("eqs", 128 * b, 128 * b + 128), v("xq"), v("xqs"))

        def half(b):
            act(v("fh%d" % b), v("b%d" % b), 0.5)

        score(0, "b4", 0, 256)
        score(0, "b5", 256, 512)
        if r == 0:
            upick(1, 4)
        ts(v("sw0", 0, 256), v("b4", 0, 256), -1.0, OP.mult)
        act(v("sw0", 256, 512), v("b5", 0, 256), -1.0)
        fit(3)
        vgather(v("g0"), v("sw0"), v("tb"))
        fit(3)
        score(1, "b6")
        scored(1, "b6")
        sgather(v("o1"), v("sw1"), v("tb"))

        def tail(k, part):
            dst = "idw" if k == 4 else "id%dr" % (k + 1)
            if part == 0:
                scatter(v(dst), v("rk"), v("id%dr" % k))
            elif part == 1:
                scan(v("ds", 0, 64), v("md", 0, 64), v(dst), 0.0, OP.mult, OP.add)
            else:
                tab = "tab5" if k == 4 else "tbl%d" % k
                ts(v(tab), compact(64), dsc, OP.mult)
                sgather(v("o%d" % (k + 2)), v("sw%d" % (k + 2)), v(tab))
                act(v("lr", 4 * k, 4 * k + 4), compact(64))
                dma("y", "dga%d%d" % (r, k), 1, ("dg%d" % r, 0, 128, k, k + 1, dg[k]), v("lr", 4 * k, 4 * k + 4))

        for k in range(5):
            w = WID[k]
            G = v("g%d" % k)
            C = "c%d" % k
            if k < 3:
                tt(v("gm"), G, v("mq%d" % k), OP.max)
                scan(v("kk"), v("rst%d" % k), G, BIG, OP.max, OP.min)
                if k:
                    tail(k - 1, 0)
                scan(v("kd"), v("rst3"), v("gm"), BIG, OP.max, OP.min)
            else:
                scan(v("kk"), v("rst%d" % k), G, BIG, OP.max, OP.min)
                tail(k - 1, 0)
                scan(v("kd"), v("mh"), v("kk"), BIG, OP.min, OP.max)
            if k:
                tail(k - 1, 1)
            fit(3)
            s = 17 if k < 3 else w + 1
            for c in range(4):
                x = v("kd", 16 * c + 15, 16 * c + 16)
                if k < 3:
                    ts(v(C, s * c, s * c + 16), v("kk", 16 * c, 16 * c + 16), x, OP.subtract, th[k], OP.is_gt)
                else:
                    left = c % 2 == 0 if k == 3 else c < 2
                    a = 16 * (c ^ 1) if k == 3 else 32 * left
                    ts(v(C, s * c, s * c + w), v("kk", a, a + w), x, OP.is_gt if left else OP.is_ge)
            if k:
                tail(k - 1, 2)
            scan(v("sm", 0, 4 * s), v(("ms%d" if k < 3 else "msk%d") % k), v(C), 0.0, OP.mult, OP.add)
            fit(4)
            if k < 3:
                ts(v("rk"), v("sm", 16, 68, 17), 1.0 / SEP, OP.mult)
            else:
                copy(v("rk"), v("sm", w, 4 * s, s))
            fit(4)
            scatter(v("g%d" % (k + 1)), v("rk"), v("o%d" % (k + 1)))
            fit(99)
            if r == 0:
                if k == 0:
                    score(2, "b7")
                    score(3, "b4")
                    scored(2, "b7")
                    scored(3, "b4")
                    masks(2)
                    later(upick, 4, 5)
                    masks3()
                elif k == 1:
                    score(4, "b5")
                    scored(4, "b5")
                    later(upick, 5, 6)
                    masks4()
                    units(0)
                    units(1)
                elif k == 2:
                    score(5, "b6")
                    scored(5, "b6")
                    unpack(0)
                    later(upick, 6, 8)
                    units(2)
                    units(3)
                elif k == 3:
                    score(6, "b7")
                    scored(6, "b7")
                    score(7, "b4")
                    for b in range(1, 4):
                        unpack(b)
                    masks5()
                else:
                    scored(7, "b4")
                    half(0)
            elif k == 0:
                score(2, "b7")
                scored(2, "b7")
                score(3, "b4")
                for b in range(4):
                    unpack(b)
                    if b < 3:
                        score(b + 4, "b%d" % (b + 5))
                scored(3, "b4")
                score(7, "b4")
                half(0)
            elif k < 3:
                scored(k + 3, "b%d" % (k + 4))
                half(k)
            elif k == 3:
                scored(6, "b7")
                scored(7, "b4")

        def runmin(out, a, b=None):
            scan(out, a, b or a, BIG, OP.min, OP.min)

        def hold(w):
            if w == 64:
                scan(v("hh"), v("mh"), v("no", 0, 64), BIG, OP.min, OP.max)
            else:
                for a in range(4):
                    c = 64 * (a % (w // 64))
                    scan(quad("hh", 0, 64, a), quad("mh", 0, 64, a), quad("no", c, c + 64, a), BIG, OP.min, OP.max)

        def versus(k, w, c):
            s = w + 1
            ts(v("c%d" % k, s * c, s * c + w), v("np", 0, w), v("hh", 16 * c + 15, 16 * c + 16), OP.subtract, th[k], OP.is_gt)
            if k > 5:
                accum(v("jk", s * c, s * c + s), v("c%d" % k, s * c, s * c + s), v("sum4", c, c + 1))

        def swap1(out, in_, n, src=quad):
            for a in range(4):
                o, i = quad(out, 0, n, a), src(in_, 0, n, a ^ 1)
                if a < 2:
                    copy(o, i)
                else:
                    act(o, i)

        def dsq(_n, c0, n, a):
            return compact(16 * n, 32 * a, 32 * a + 32)

        def swap2(out, in_, n):
            copy(v(out, 0, n, 1, 0, 64), v(in_, 0, n, 1, 64, 128))
            act(v(out, 0, n, 1, 64, 128), v(in_, 0, n, 1, 0, 64))

        def owns(name, src, per):
            for a in range(4):
                c = 4 * (a % per)
                ts(quad(name, 0, 4, a), quad(src, c, c + 4, a), dscp(32 * a, 32 * a + 32), OP.mult)

        runmin(v("no", 0, 64), v("g5"))
        tail(4, 0)
        swap1("np", "no", 64)
        hold(64)
        tail(4, 1)
        for c in range(4):
            versus(5, 64, c)
        tail(4, 2)
        fit(99)
        if r == 0:
            places(128, 512)
            later(quant, v("vq"), v("vqs"), v("vt"))
        scan(v("sm"), v("msk5"), v("c5"), 0.0, OP.mult, OP.add)
        copy(v("rk"), v("sm", 64, 260, 65))
        fit(3)
        scatter(v("w5s%d" % r), v("rk"), v("o6"))
        swap1("shs", "w5s%d" % r, 128)
        scatter(v("w5%d" % r), v("rk"), v("idw"))
        runmin(v("no", 0, 128), v("w5s%d" % r), v("shs"))
        scan(v("ds", 0, 128), v("md", 0, 128), v("w5%d" % r), 0.0, OP.mult, OP.add)
        swap2("np", "no", 128)
        fit(3)
        hold(128)
        swap1("sh", "ds", 8, dsq)
        versus(6, 128, 0)
        versus(6, 128, 1)
        tt(v("a5"), compact(128), v("sh", 0, 8), OP.add)
        versus(6, 128, 2)
        versus(6, 128, 3)
        owns("own6", "a5", 2)
        fit(8)
        sgather(v("id6"), v("iot"), v("own6"))
        ts(v("rk"), v("sum4"), 1.0, OP.mult)
        scatter(v("w6%d" % r), v("rk"), v("id6"))
        for B in range(4):
            h = 16 * (4 * (B % 2) + B // 2)
            dma("y", "dm%d" % r, 4, v(lst, 8 * B, 8 * B + 8, 1, 80, 96), v("a5", 0, 8, 1, h, h + 16))
        for B in range(8):
            h = 16 * group_of(B)
            dma("y", "dl%d" % r, 8, v(lst, 4 * B, 4 * B + 4, 1, 0, 80), ("dg%d" % r, h, h + 16, 0, 5, dg[0:5, h:h + 16, :]))
        fit(99)
        scan(v("ds", 0, 256), v("md", 0, 256), v("w6%d" % r), 0.0, OP.mult, OP.add)
        swap1("sh", "ds", 16, dsq)
        tt(v("ap6", 0, 16), compact(256), v("sh", 0, 16), OP.add)
        trans(v("tr"), v("ap6"))
        swap2("sh", "tr", 32)
        tt(v("sw", 32, 48), v("tr", 16, 32), v("sh", 16, 32), OP.add)
        tt(v("sw", 48, 64), v("tr", 0, 16), v("sh", 0, 16), OP.add)
        tt(v("sw", 0, 32), v("tr"), v("sh"), OP.add)
        trans(v("tr2"), v("sw"))
        ts(v("tab7", 16, 32), v("tr2", 32, 48), dsc, OP.mult)
        ts(v("tab7", 0, 16), v("tr2", 0, 16), dsc, OP.mult)
        for j in range(2):
            dma("y", "dn%d" % r, 2, v(lst, 16 * j, 16 * j + 16, 1, 96, 112), v("tr2", 0, 16, 1, 16 * j, 16 * j + 16))
        sgather(v("gg", 256, 512), v("sw7"), v("tab7", 16, 32))
        vgather(v("gg", 0, 256), v("sw7"), v("tab7", 0, 16))
        owns("own7", "tr2", 4)
        sgather(v("id7"), v("iot"), v("own7"))
        runmin(v("no"), v("gg", 0, 256))
        runmin(v("np"), v("gg", 256, 512))
        hold(256)
        for c in range(4):
            versus(7, 256, c)
        if r == 0:
            half(1)
            half(2)
        half(3)
        ts(v("rk"), v("sum4"), 1.0, OP.mult)
        scatter(v("w7%d" % r), v("rk"), v("id7"))
        ts(v("off", 0, 32, 1, 0, 96), v(lst, 0, 32, 1, 0, 96), dscp(0, 96), OP.mult)
        trans(quad("tl", 0, 32, 3), quad(lst, 0, 32, 3))
        scan(v("ds"), v("md"), v("w7%d" % r), 0.0, OP.mult, OP.add)
        copy(quad("qe", 0, 16, 3), quad("tl", 0, 16, 3))
        tt(v("qa", 0, 32, 1, 64, 128), compact(512, 64, 128), compact(512, 0, 64), OP.add)
        tt(quad("qb", 0, 32, 3), quad("qa", 0, 32, 3), quad("qa", 0, 32, 2), OP.add)
        trans(quad("qt", 0, 32, 3), quad("qb", 0, 32, 3))
        tt(quad("qe", 16, 32, 3), quad("qt", 0, 16, 3), quad("qt", 16, 32, 3), OP.add)
        trans(quad("tr7", 0, 32, 3), quad("qe", 0, 32, 3))
        ts(quad("off", 0, 32, 3), quad("tr7", 0, 32, 3), dscp(96, 128), OP.mult)
        for b in range(1, 4):
            sgather(v("pa%d" % b), v("fh%d" % b), v("off", 0, 16))
        vgather(v("pa0"), v("fh0"), v("off", 0, 16))
        for b in (1, 0, 2, 3):
            ttg(v("zt", b, 1024, 4), v("fh%d" % b), v("off", 16, 32), v("pa%d" % b))
        quant(v("zq"), v("zqs"), v("zt"))
        rid, pid, _s = topo.addr(nxt)
        eng = topo.engines(core, nxt)
        for src, land, sem, loc, es in ((cd("zq"), cd("zl%d" % r), "ac%d" % r, "lc%d" % r, eng[0::2]),
                                        (v("zqs"), v("zl%ds" % r), "as%d" % r, "ls%d" % r, eng[1::4])):
            deps("g", [src], [])
            g.remote_dma(land[5], src[5], T.sem[sem], T.sem[loc], pid, rid, sum(1 << e for e in es))
            total[sem] = total[loc] = len(es)
            note("g", (loc, len(es)), [src], [])
            note("x", (sem, len(es)), [], [land])
        if r < R - 1:
            for B in range(8):
                h = 16 * group_of(B)
                dma("y", "db%d" % r, 8, v("tbf", 0, 4, 1, h, h + 16), v("tr7", 4 * B, 4 * B + 4, 1, 112, 128))
        act(v("f0"), v("b0"))
        act(v("f1"), v("b1"))
        scatter(v("posw"), v("off"), v("iotm"))
        scan(v("pds"), v("md"), v("posw"), 0.0, OP.mult, OP.add)
        ts(v("pos"), v("pds", 15, 512, 16), dsc, OP.mult)
        if r == R - 1:
            sgather(v("row"), v("iot"), v("off"))
            dma("y", "dod", 1, ("od", 0, 8, 0, 512, T.od[:, :]), ("row", 0, 128, 0, 512, T.row[0:128:16, :]))
        for b in (0, 2, 1, 3):
            mm(v("b%d" % (4 + b), 0, 256), v("wq", 128 * b, 128 * b + 128), v("wqs", 128 * b, 128 * b + 128), v("zl%d" % r), v("zl%ds" % r))
        for b in (2, 3):
            act(v("pp%d" % b), v("b%d" % (4 + b), 0, 256), 0.03125)
        for b in (0, 1):
            ts(v("pp%d" % b), v("b%d" % (4 + b), 0, 256), 0.03125, OP.mult)
        for b in (2, 3):
            sgather(v("gp%d" % b), v("pp%d" % b), v("pos"))
        for b in (0, 1):
            ttg(v("xt", b, 2048, 4), v("pp%d" % b), v("pos"), v("f%d" % b))
        for b in (2, 3):
            for c in (0, 256):
                tt(v("xt", 4 * c + b, 4 * c + 1024, 4), v("gp%d" % b, c, c + 256), v("b%d" % b, c, c + 256), OP.add)

    for c in (0, 256):
        quant(v("xq", c, c + 256), v("xqs", c, c + 256), v("xt", 4 * c, 4 * c + 1024))
        mm(v("b4" if c == 0 else "b5", 0, 256), v("vq"), v("vqs"), v("xq", c, c + 256), v("xqs", c, c + 256))
    dma("y", "doc", 1, ("oc", 0, 128, 0, 2048, T.oc[:, :]), cd("xq"))
    for k in range(4):
        dma("y", "dos", 4, ("osc", 4 * k, 4 * k + 4, 0, 512, T.osc[4 * k:4 * k + 4, :]), v("xqs", 0, 512, 1, 32 * k, 32 * k + 4))
    copy(v("yy", 0, 256), v("b4", 0, 256))
    act(v("yy", 256, 512), v("b5", 0, 256))
    dma("y", "dy", 1, ("y", 0, 128, 0, 512, T.y[:, :]), v("yy"))
    for k in semof:
        need("g", (semof[k], count[k]))
    for s in total:
        need("g", (s, total[s]))
